import numpy as np
import ml_dtypes


def mxq(x, axis, fmt="e4m3"):
    dtype, down = {"e4m3": (ml_dtypes.float8_e4m3fn, 7), "e5m2": (ml_dtypes.float8_e5m2, 14)}[fmt]
    v = np.moveaxis(np.asarray(x, np.float32).astype(ml_dtypes.bfloat16).astype(np.float64), axis, -1)
    blocks = v.reshape(v.shape[:-1] + (-1, 32))
    amax = np.abs(blocks).max(-1, keepdims=True)
    byte = np.maximum(np.where(amax > 0, np.frexp(amax)[1] - 1 + 127, 0) - down, 1)
    scale = np.exp2(byte - 127.0)
    codes = (blocks / scale).astype(np.float32).astype(dtype).astype(np.float64)
    return np.moveaxis((codes * scale).reshape(v.shape), -1, axis)


WIDE = False


def mx_kscale(k):
    if not WIDE:
        return np.ones(k)
    levels = np.array([10, -10, 5, -5, 0])
    if k % 512:
        return np.exp2(np.random.permutation(np.resize(levels, k // 32))).repeat(32)
    a = np.empty((k // 512, 16))
    for p in range(k // 512):
        a[p, :8] = np.random.permutation(np.resize(levels, 8))
        for g in range(8):
            far = levels[np.abs(levels - a[p, g]) >= 10]
            a[p, g + 8] = far[np.random.randint(len(far))]
    return np.exp2(a.ravel()).repeat(32)


def f64(x):
    return np.asarray(x).astype(np.float64)


def striped(idx):
    return np.tile(idx.reshape(-1, 16).T, (8, 1)).astype(np.uint16)


def unstriped(offs):
    return offs[:16].T.reshape(-1).astype(np.int64)


E2M1 = np.array([0.0, 0.5, 1.0, 1.5, 2.0, 3.0, 4.0, 6.0, -0.0, -0.5, -1.0, -1.5, -2.0, -3.0, -4.0, -6.0])


def pack_weight(w, fmt):
    k, n = w.shape
    w = f64(np.asarray(w, np.float32).astype(ml_dtypes.bfloat16)).reshape(k // 32, 32, n)
    amax = np.abs(w).max(1)
    if fmt == "e4m3":
        byte = np.frexp(amax)[1] - 1 + 127 - 7
    else:
        mant, ex = np.frexp(amax / 6.0)
        byte = np.where(mant > 0.5, ex, ex - 1) + 127
    byte = np.clip(np.where(amax > 0, byte, 1), 1, 254)
    scaled = (w * np.exp2(127.0 - byte)[:, None, :]).reshape(k, n).astype(np.float32)
    by_word = np.ascontiguousarray(scaled.reshape(k // 512, 128, 4, n).transpose(0, 1, 3, 2))
    if fmt == "e4m3":
        words = by_word.astype(ml_dtypes.float8_e4m3fn).view(np.uint8)
    else:
        c = by_word.astype(ml_dtypes.float4_e2m1fn).view(np.uint8) & 0xF
        words = (c[..., 0::2] | (c[..., 1::2] << 4)).reshape(k // 512, 128, 2 * n)
    return np.ascontiguousarray(words), np.ascontiguousarray(byte.astype(np.uint8).reshape(k // 512, 16, n))


def unpack_weight(words, scales, fmt):
    g, _, n = scales.shape
    words = np.ascontiguousarray(words).reshape(g, 128, n, -1)
    if fmt == "e4m3":
        vals = words.view(ml_dtypes.float8_e4m3fn).astype(np.float64)
    else:
        nib = np.empty((g, 128, n, 4), np.uint8)
        nib[..., 0::2] = words & 0xF
        nib[..., 1::2] = words >> 4
        vals = E2M1[nib]
    vals = vals * np.repeat(np.exp2(scales.astype(np.float64) - 127.0), 8, axis=1)[..., None]
    return vals.transpose(0, 1, 3, 2).reshape(g * 512, n)


def gelu(v):
    return 0.5 * v * (1.0 + np.tanh(np.sqrt(2.0 / np.pi) * (v + 0.044715 * v**3)))


def striped8(idx):
    return np.concatenate([v.reshape(-1, 16).T for v in idx]).astype(np.uint16)


def unstriped8(offs):
    return np.stack([offs[16 * g:16 * g + 16].T.reshape(-1) for g in range(8)]).astype(np.int64)


def runs(v, idx8):
    k = np.arange(v.shape[0])
    return v[k[:, None], idx8[k % 512 // 64]]


def bf(x):
    return np.asarray(x, np.float32).astype(ml_dtypes.bfloat16)


def planes(Y):
    n, m = Y.shape
    b = f64(bf(Y)).reshape(n // 32, 32, m)
    amax = np.abs(b).max(1)
    byte = np.clip(np.where(amax > 0, np.frexp(amax)[1] - 1 + 127 - 7, 1), 1, 254)
    codes = (b * np.exp2(127.0 - byte)[:, None, :]).reshape(n, m).astype(np.float32).astype(ml_dtypes.float8_e4m3fn).view(np.uint8)
    words = codes.reshape(n // 512, 128, 4, m).transpose(0, 1, 3, 2)
    return np.ascontiguousarray(words), np.ascontiguousarray(byte.astype(np.uint8).reshape(n // 512, 16, m))


K, H, N, T, S, P, G, R = 1024, 1024, 1024, 4096, 1024, 512, 8, 64

def setup_inputs():
    n = np.random.standard_normal
    s = mx_kscale(K)[:, None]
    u = mx_kscale(H)[:, None]
    tab_words, tab_scales = pack_weight(n((K, T)) * s, "e4m3")
    w1 = 0.85 * n((K, H)) / np.sqrt(K) / s
    w2_words, w2_scales = pack_weight(0.34 * n((H, N)) / np.sqrt(H) / u, "e2m1")
    w3 = 1.1 * n((H, N)) / np.sqrt(H) / u * np.exp(0.8 * n(N))[None, :]
    idx8 = np.stack([np.random.permutation(S)[:P] for _ in range(G)])
    return {
        "tab_words": tab_words, "tab_scales": tab_scales,
        "offs": striped(np.random.permutation(T)[:S]),
        "offs2": striped8(idx8),
        "w1": w1.astype(np.float32),
        "sky": np.random.uniform(0.3, 1.6, (H, S)).astype(np.float32),
        "slope": np.repeat(np.random.uniform(0.6, 3.0, H // R), R).astype(np.float32),
        "thr": np.repeat(n(H // R), R).astype(np.float32),
        "plan": (1.5 * n((H, P)) * u).astype(np.float32),
        "w2_words": w2_words, "w2_scales": w2_scales,
        "weather": np.random.uniform(-1.4, 1.4, (N, P)).astype(np.float32),
        "w3": w3.astype(np.float32),
    }

def reference(tab_words, tab_scales, offs, offs2, w1, sky, slope, thr, plan,
              w2_words, w2_scales, weather, w3):
    v = unpack_weight(tab_words, tab_scales, "e4m3")[:, unstriped(offs)]
    h = (mxq(f64(w1), 0, "e4m3").T @ v) * f64(sky)
    hp = runs(h, unstriped8(offs2))
    a = 1.0 / (1.0 + np.exp(-(f64(slope)[:, None] * hp + f64(thr)[:, None])))
    x = mxq(a * f64(plan), 0, "e4m3")
    w2 = unpack_weight(w2_words, w2_scales, "e2m1")
    e = w2.T @ x
    d = mxq(f64(w3), 0, "e4m3").T @ x
    y = np.sin(e + f64(weather)) * d
    words, scales = planes(y)
    return y, words, scales

@@ -1,0 +1,299 @@
+import math
+from contextlib import ExitStack
+
+import concourse.mybir as mybir
+
+K, H, N, T, S, M = 1024, 1024, 1024, 4096, 1024, 512
+FLOPS = 2 * K * H * S + 2 * 2 * H * N * M
+
+F32 = mybir.dt.float32
+BF16 = mybir.dt.bfloat16
+I32 = mybir.dt.int32
+U32 = mybir.dt.uint32
+U16 = mybir.dt.uint16
+U8 = mybir.dt.uint8
+FP8X4 = mybir.dt.float8_e4m3fn_x4
+FP4X4 = mybir.dt.float4_e2m1fn_x4
+ALU = mybir.AluOpType
+ACT = mybir.ActivationFunctionType
+
+P = 128
+PACK = 4
+GROUP = P * PACK
+BANK = 512
+HALF = M // 2
+
+
+def tile_list_pass_tile_scores_kernel(
+    tc, tab_words, tab_scales, offs, offs2, w1, sky, slope, thr, plan,
+    w2_words, w2_scales, weather, w3, out_0, out_1, out_2,
+):
+    nc = tc.nc
+    with ExitStack() as ctx:
+        keep = ctx.enter_context(tc.tile_pool(name="keep", bufs=1))
+        psum = ctx.enter_context(tc.psum_pool(name="psum", bufs=8))
+
+        def dealt_rows(src, g):
+            return src[GROUP * g : GROUP * (g + 1), :].rearrange("(p i) c -> p i c", i=PACK)
+
+        pass_list = keep.tile([P, S // 16], U16, name="pass_list")
+        nc.sync.dma_start(pass_list[:], offs)
+        look_lists = keep.tile([P, M // 16], U16, name="look_lists")
+        nc.sync.dma_start(look_lists[:], offs2)
+
+        tab_plane = keep.tile([P, T], U8, name="tab_plane", tag="tab_plane", align_bytes=64)
+        nc.vector.memset(tab_plane[:].bitcast(I32), 0)
+        slope_sb = keep.tile([P, 2, PACK], F32, name="slope_sb")
+        nc.sync.dma_start(slope_sb[:], slope.rearrange("(b p i) -> p b i", b=2, i=PACK))
+        thr_sb = keep.tile([P, 2, PACK], F32, name="thr_sb")
+        nc.sync.dma_start(thr_sb[:], thr.rearrange("(b p i) -> p b i", b=2, i=PACK))
+        w2_plane_raw = keep.tile([P, 2 * N], U8, name="w2_plane_raw", align_bytes=64)
+        nc.vector.memset(w2_plane_raw[:].bitcast(I32), 0)
+        w2_raw = keep.tile([P, 2 * 2 * N], U8, name="w2_raw", align_bytes=64)
+        for a in range(2):
+            nc.sync.dma_start(w2_raw[:, 2 * N * a : 2 * N * (a + 1)].bitcast(I32), w2_words[a].bitcast(I32))
+
+        def load_table(a, pieces):
+            t = keep.tile([P, T], I32, name="table", tag="table", bufs=2, align_bytes=64)
+            src = tab_words[a].rearrange("p n i -> p (n i)").bitcast(I32)
+            for u in range(pieces):
+                cols = slice(u * T // pieces, (u + 1) * T // pieces)
+                nc.sync.dma_start(t[:, cols], src[:, cols])
+            return t
+
+        def load_weight(w, a, g, tag):
+            t = keep.tile([P, PACK, GROUP], F32, name=tag, tag=tag, bufs=4, align_bytes=64)
+            nc.sync.dma_start(t[:], dealt_rows(w, a)[:, :, GROUP * g : GROUP * (g + 1)])
+            return t
+
+        def load_sky(b, i):
+            t = keep.tile([P, S], F32, name="rows", tag="rows", bufs=8, align_bytes=64)
+            nc.sync.dma_start(t[:], dealt_rows(sky, b)[:, i, :])
+            return t
+
+        def load_matrix(src, g, tag):
+            t = keep.tile([P, PACK, M], F32, name=tag, tag=tag, bufs=2, align_bytes=64)
+            nc.sync.dma_start(t[:], dealt_rows(src, g))
+            return t
+
+        table, w1_raw, w3_raw, h, plan_sb, z = {}, {}, {}, {}, {}, {}
+        table[0] = load_table(0, 2)
+        for q in range(4):
+            nc.sync.dma_start(
+                tab_plane[32 * q : 32 * q + 8, :].bitcast(I32),
+                tab_scales[:, 4 * q : 4 * q + 4, :].bitcast(I32),
+            )
+        w1_raw[0, 0] = load_weight(w1, 0, 0, "w1_raw")
+        for q in range(4):
+            nc.sync.dma_start(
+                w2_plane_raw[32 * q : 32 * q + 4, :].bitcast(I32).rearrange("r (a n) -> r a n", a=2),
+                w2_scales[:, 4 * q : 4 * q + 4, :].bitcast(I32).rearrange("a r n -> r a n"),
+            )
+
+        table[1] = load_table(1, 1)
+        w1_raw[1, 0] = load_weight(w1, 1, 0, "w1_raw")
+        h[0, 0] = load_sky(0, 0)
+        h[0, 1] = load_sky(0, 1)
+        w1_raw[0, 1] = load_weight(w1, 0, 1, "w1_raw")
+        h[0, 2] = load_sky(0, 2)
+        w1_raw[1, 1] = load_weight(w1, 1, 1, "w1_raw")
+        h[0, 3] = load_sky(0, 3)
+        for i in range(PACK):
+            h[1, i] = load_sky(1, i)
+        for b in range(2):
+            plan_sb[b] = load_matrix(plan, b, "plan_sb")
+        w3_raw[0, 0] = load_weight(w3, 0, 0, "w3_raw")
+        z[0] = load_matrix(weather, 0, "z")
+        w3_raw[1, 0] = load_weight(w3, 1, 0, "w3_raw")
+        z[1] = load_matrix(weather, 1, "z")
+        for a in range(2):
+            w3_raw[a, 1] = load_weight(w3, a, 1, "w3_raw")
+
+        w2_codes = keep.tile([P, 2 * 2 * N], U8, name="w2_codes", align_bytes=64)
+        nc.vector.tensor_copy(
+            w2_codes[:].rearrange("p (u t c e) -> p u c t e", u=4, t=PACK, e=2),
+            w2_raw[:].rearrange("p (u c t e) -> p u c t e", u=4, t=PACK, e=2),
+        )
+
+        v_codes = {}
+
+        def gather_words(a, half, tag):
+            entries = pass_list[:, 32 * half : 32 * (half + 1)]
+            v_codes[a, half] = keep.tile([P, BANK], U32, name=tag, tag=tag, align_bytes=64)
+            nc.vector.tensor_copy(v_codes[a, half][:], table[a][:].bitcast(U32).indirect(entries))
+
+        def stage_tile():
+            return keep.tile([P, PACK * GROUP], BF16, name="stage", tag="stage", bufs=4, align_bytes=64)
+
+        def round_weight(raw, scalar_share):
+            staged = stage_tile()
+            dst = staged[:].rearrange("p (t c j) -> p c j t", t=PACK, j=PACK)
+            src = raw[:].rearrange("p j (c t) -> p c j t", t=PACK)
+            if scalar_share > 0:
+                nc.scalar.copy(dst[:, :scalar_share], src[:, :scalar_share])
+            if scalar_share < P:
+                nc.vector.tensor_copy(dst[:, scalar_share:], src[:, scalar_share:])
+            return staged
+
+        def quantize(staged, width, name):
+            codes = keep.tile([P, width], U32, name=name + "_codes", align_bytes=64)
+            plane = keep.tile([P, width], U8, name=name + "_plane", align_bytes=64)
+            nc.vector.quantize_mx(out=codes[:].bitcast(FP8X4), scales=plane[:], in_=staged[:, : PACK * width])
+            return codes, plane
+
+        w1q, w3q, xq = {}, {}, {}
+        on_s, on_v = nc.scalar.copy, nc.vector.tensor_copy
+        gather_words(0, 0, "v00")
+        gather_words(0, 1, "v01")
+        v_plane = keep.tile([P, S], U8, name="v_plane", align_bytes=64)
+        nc.vector.tensor_copy(v_plane[:], tab_plane[:].indirect(pass_list[:]))
+        w2_plane = keep.tile([P, 2 * N], U8, name="w2_plane", align_bytes=64)
+        nc.vector.tensor_copy(
+            w2_plane[:].rearrange("p (u t c) -> p u c t", u=4, t=PACK),
+            w2_plane_raw[:].rearrange("p (u c t) -> p u c t", u=4, t=PACK),
+        )
+        w1q[0, 0] = quantize(round_weight(w1_raw[0, 0], P), GROUP, "w1_00")
+        gather_words(1, 0, "tab_plane")
+        gather_words(1, 1, "v11")
+        w1q[1, 0] = quantize(round_weight(w1_raw[1, 0], 48), GROUP, "w1_10")
+
+        looks = {}
+
+        sums = {}
+
+        def first_pass(b, i, half, a):
+            cols = slice(P * i, P * (i + 1))
+            js = slice(BANK * half, BANK * (half + 1))
+            if a == 0:
+                sums[b, i, half] = psum.tile([P, BANK], F32, name="bank", tag="bank")
+            codes, plane = w1q[a, b]
+            nc.tensor.matmul_mx(
+                out=sums[b, i, half][:], lhsT=codes[:, cols].bitcast(FP8X4), lhsT_scale=plane[:, cols],
+                rhs=v_codes[a, half][:].bitcast(FP8X4), rhs_scale=v_plane[4 * a :, js],
+                start=(a == 0), stop=(a == 1),
+            )
+
+        def first_stage(b, i):
+            for half in range(2):
+                js = slice(BANK * half, BANK * (half + 1))
+                if b == 1:
+                    first_pass(b, i, half, 0)
+                first_pass(b, i, half, 1)
+                nc.vector.tensor_tensor(h[b, i][:, js], sums[b, i, half][:], h[b, i][:, js], ALU.mult)
+            if i == 0:
+                looks[b] = keep.tile([P, PACK, M], F32, name="looks", tag="table", bufs=2, align_bytes=64)
+            nc.scalar.activation(
+                out=looks[b][:, i, :], in_=h[b, i][:].indirect(look_lists[:]), func=ACT.Sigmoid,
+                bias=thr_sb[:, b, i : i + 1], scale=slope_sb[:, b, i : i + 1],
+            )
+
+        def make_x(b, half):
+            ms = slice(HALF * half, HALF * (half + 1))
+            staged = stage_tile()
+            nc.vector.tensor_tensor(
+                staged[:, : PACK * HALF].rearrange("p (c k i) -> p c i k", i=PACK, k=4),
+                looks[b][:, :, ms].rearrange("p i (c k) -> p c i k", k=4),
+                plan_sb[b][:, :, ms].rearrange("p i (c k) -> p c i k", k=4),
+                ALU.mult,
+            )
+            return staged
+
+        for i in range(PACK):
+            for half in range(2):
+                first_pass(0, i, half, 0)
+        first_stage(0, 0)
+        staged = round_weight(w1_raw[0, 1], P)
+        first_stage(0, 1)
+        w1q[0, 1] = quantize(staged, GROUP, "w1_01")
+        first_stage(0, 2)
+        staged = round_weight(w1_raw[1, 1], P)
+        first_stage(0, 3)
+        w1q[1, 1] = quantize(staged, GROUP, "w1_11")
+        for i in range(PACK):
+            first_stage(1, i)
+        for b in range(2):
+            staged = [make_x(b, half) for half in range(2)]
+            for half in range(2):
+                xq[b, half] = quantize(staged[half], HALF, f"x_{b}{half}")
+
+        y_plane = keep.tile([P, 2, M], U8, name="y_plane", align_bytes=64)
+        sines, squares = {}, {}
+
+        def phase(g, half):
+            ms = slice(HALF * half, HALF * (half + 1))
+            for pair in range(2):
+                acc = psum.tile([P, 2, HALF], F32, name="bank", tag="bank")
+                for k in range(2):
+                    t = 2 * pair + k
+                    for a in range(2):
+                        col = N * a + GROUP * g + P * t
+                        codes, plane = xq[a, half]
+                        nc.tensor.matmul_mx(
+                            out=acc[:, k, :], lhsT=w2_codes[:, 2 * col : 2 * (col + P)].bitcast(FP4X4),
+                            lhsT_scale=w2_plane[:, col : col + P],
+                            rhs=codes[:].bitcast(FP8X4), rhs_scale=plane[:],
+                            start=(a == 0), stop=(a == 1),
+                        )
+                rows = z[g][:, 2 * pair : 2 * pair + 2, ms]
+                nc.vector.scalar_tensor_tensor(rows, acc[:], math.pi / 2, rows, ALU.add, ALU.add)
+            s = keep.tile([P, PACK, HALF], F32, name="sines", tag="rows", bufs=8, align_bytes=64)
+            nc.scalar.activation(out=s[:], in_=z[g][:, :, ms], func=ACT.Sin, scale=0.5)
+            q = keep.tile([P, PACK, HALF], F32, name="squares", tag="rows", bufs=8, align_bytes=64)
+            nc.scalar.activation(out=q[:], in_=s[:], func=ACT.Square, scale=math.sqrt(2.0))
+            sines[g, half], squares[g, half] = s, q
+
+        def amplitude(g, half):
+            ms = slice(HALF * half, HALF * (half + 1))
+            s, q = sines[g, half], squares[g, half]
+            for pair in range(2):
+                acc = psum.tile([P, 2, HALF], F32, name="bank", tag="bank")
+                for k in range(2):
+                    cols = slice(P * (2 * pair + k), P * (2 * pair + k + 1))
+                    for a in range(2):
+                        w_codes, w_plane = w3q[a, g]
+                        codes, plane = xq[a, half]
+                        nc.tensor.matmul_mx(
+                            out=acc[:, k, :], lhsT=w_codes[:, cols].bitcast(FP8X4), lhsT_scale=w_plane[:, cols],
+                            rhs=codes[:].bitcast(FP8X4), rhs_scale=plane[:],
+                            start=(a == 0), stop=(a == 1),
+                        )
+                rows = q[:, 2 * pair : 2 * pair + 2, :]
+                nc.vector.scalar_tensor_tensor(rows, rows, 1.0, acc[:], ALU.subtract, ALU.mult)
+            nc.sync.dma_start(dealt_rows(out_0, g)[:, :, ms], q[:])
+
+        def planes(g, half, copy):
+            ms = slice(HALF * half, HALF * (half + 1))
+            staged = stage_tile()
+            copy(
+                staged[:, : PACK * HALF].rearrange("p (c k t) -> p c t k", t=PACK, k=4),
+                squares[g, half][:].rearrange("p t (c k) -> p c t k", k=4),
+            )
+            codes = keep.tile([P, HALF], U32, name=f"y_codes{g}{half}", align_bytes=64)
+            nc.vector.quantize_mx(out=codes[:].bitcast(FP8X4), scales=y_plane[:, g, ms], in_=staged[:, : PACK * HALF])
+            nc.sync.dma_start(
+                out_1[g].rearrange("p m t -> p (m t)").bitcast(I32)[:, ms], codes[:].bitcast(I32)
+            )
+
+        staged = round_weight(w3_raw[0, 0], P)
+        phase(0, 0)
+        phase(0, 1)
+        w3q[0, 0] = quantize(staged, GROUP, "w3_00")
+        w3q[1, 0] = quantize(round_weight(w3_raw[1, 0], P), GROUP, "w3_10")
+        phase(1, 0)
+        staged = round_weight(w3_raw[0, 1], P)
+        phase(1, 1)
+        amplitude(0, 0)
+        amplitude(0, 1)
+        w3q[0, 1] = quantize(staged, GROUP, "w3_01")
+        w3q[1, 1] = quantize(round_weight(w3_raw[1, 1], 0), GROUP, "w3_11")
+        planes(0, 0, on_s)
+        planes(0, 1, on_s)
+        amplitude(1, 0)
+        amplitude(1, 1)
+        planes(1, 0, on_v)
+        planes(1, 1, on_v)
+        for q in range(4):
+            nc.sync.dma_start(
+                out_2[:, 4 * q : 4 * q + 4, :].bitcast(I32).rearrange("g r m -> r g m"),
+                y_plane[32 * q : 32 * q + 4, :, :].bitcast(I32),
+            )

@@ -41,17 +41,24 @@ def tile_list_pass_tile_scores_kernel(
         look_lists = keep.tile([P, M // 16], U16, name="look_lists")
         nc.sync.dma_start(look_lists[:], offs2)
 
+        w2_plane_raw = keep.tile([P, 2 * N], U8, name="w2_plane_raw", align_bytes=64)
+        nc.gpsimd.memset(w2_plane_raw[:].bitcast(I32), 0)
         tab_plane = keep.tile([P, T], U8, name="tab_plane", tag="tab_plane", align_bytes=64)
         nc.vector.memset(tab_plane[:].bitcast(I32), 0)
+        for q in range(4):
+            nc.gpsimd.dma_start(
+                tab_plane[32 * q : 32 * q + 8, :].bitcast(I32),
+                tab_scales[:, 4 * q : 4 * q + 4, :].bitcast(I32),
+            )
         slope_sb = keep.tile([P, 2, PACK], F32, name="slope_sb")
         nc.sync.dma_start(slope_sb[:], slope.rearrange("(b p i) -> p b i", b=2, i=PACK))
         thr_sb = keep.tile([P, 2, PACK], F32, name="thr_sb")
         nc.sync.dma_start(thr_sb[:], thr.rearrange("(b p i) -> p b i", b=2, i=PACK))
-        w2_plane_raw = keep.tile([P, 2 * N], U8, name="w2_plane_raw", align_bytes=64)
-        nc.vector.memset(w2_plane_raw[:].bitcast(I32), 0)
         w2_raw = keep.tile([P, 2 * 2 * N], U8, name="w2_raw", align_bytes=64)
-        for a in range(2):
-            nc.sync.dma_start(w2_raw[:, 2 * N * a : 2 * N * (a + 1)].bitcast(I32), w2_words[a].bitcast(I32))
+        nc.sync.dma_start(
+            w2_raw[:].bitcast(I32).rearrange("p (a n) -> p a n", a=2),
+            w2_words.bitcast(I32).rearrange("a p n -> p a n"),
+        )
 
         def load_table(a, pieces):
             t = keep.tile([P, T], I32, name="table", tag="table", bufs=2, align_bytes=64)
@@ -62,7 +69,7 @@ def tile_list_pass_tile_scores_kernel(
             return t
 
         def load_weight(w, a, g, tag):
-            t = keep.tile([P, PACK, GROUP], F32, name=tag, tag=tag, bufs=4, align_bytes=64)
+            t = keep.tile([P, PACK, GROUP], F32, name=tag, tag=tag, bufs=6, align_bytes=64)
             nc.sync.dma_start(t[:], dealt_rows(w, a)[:, :, GROUP * g : GROUP * (g + 1)])
             return t
 
@@ -78,12 +85,7 @@ def tile_list_pass_tile_scores_kernel(
 
         table, w1_raw, w3_raw, h, plan_sb, z = {}, {}, {}, {}, {}, {}
         table[0] = load_table(0, 2)
-        for q in range(4):
-            nc.sync.dma_start(
-                tab_plane[32 * q : 32 * q + 8, :].bitcast(I32),
-                tab_scales[:, 4 * q : 4 * q + 4, :].bitcast(I32),
-            )
-        w1_raw[0, 0] = load_weight(w1, 0, 0, "w1_raw")
+        w1_raw[0, 0] = load_weight(w1, 0, 0, "w_raw")
         for q in range(4):
             nc.sync.dma_start(
                 w2_plane_raw[32 * q : 32 * q + 4, :].bitcast(I32).rearrange("r (a n) -> r a n", a=2),
@@ -91,23 +93,25 @@ def tile_list_pass_tile_scores_kernel(
             )
 
         table[1] = load_table(1, 1)
-        w1_raw[1, 0] = load_weight(w1, 1, 0, "w1_raw")
+        w1_raw[1, 0] = load_weight(w1, 1, 0, "w_raw")
         h[0, 0] = load_sky(0, 0)
+        w1_raw[0, 1] = load_weight(w1, 0, 1, "w_raw")
         h[0, 1] = load_sky(0, 1)
-        w1_raw[0, 1] = load_weight(w1, 0, 1, "w1_raw")
+        w1_raw[1, 1] = load_weight(w1, 1, 1, "w_raw")
         h[0, 2] = load_sky(0, 2)
-        w1_raw[1, 1] = load_weight(w1, 1, 1, "w1_raw")
         h[0, 3] = load_sky(0, 3)
-        for i in range(PACK):
-            h[1, i] = load_sky(1, i)
-        for b in range(2):
-            plan_sb[b] = load_matrix(plan, b, "plan_sb")
-        w3_raw[0, 0] = load_weight(w3, 0, 0, "w3_raw")
+        h[1, 0] = load_sky(1, 0)
+        h[1, 1] = load_sky(1, 1)
+        h[1, 2] = load_sky(1, 2)
+        h[1, 3] = load_sky(1, 3)
+        plan_sb[0] = load_matrix(plan, 0, "plan_sb")
+        plan_sb[1] = load_matrix(plan, 1, "plan_sb")
+        w3_raw[0, 0] = load_weight(w3, 0, 0, "w_raw")
         z[0] = load_matrix(weather, 0, "z")
-        w3_raw[1, 0] = load_weight(w3, 1, 0, "w3_raw")
+        w3_raw[1, 0] = load_weight(w3, 1, 0, "w_raw")
         z[1] = load_matrix(weather, 1, "z")
-        for a in range(2):
-            w3_raw[a, 1] = load_weight(w3, a, 1, "w3_raw")
+        w3_raw[0, 1] = load_weight(w3, 0, 1, "w_raw")
+        w3_raw[1, 1] = load_weight(w3, 1, 1, "w_raw")
 
         w2_codes = keep.tile([P, 2 * 2 * N], U8, name="w2_codes", align_bytes=64)
         nc.vector.tensor_copy(
@@ -123,10 +127,11 @@ def tile_list_pass_tile_scores_kernel(
             nc.vector.tensor_copy(v_codes[a, half][:], table[a][:].bitcast(U32).indirect(entries))
 
         def stage_tile():
-            return keep.tile([P, PACK * GROUP], BF16, name="stage", tag="stage", bufs=4, align_bytes=64)
+            return keep.tile([P, PACK * GROUP], BF16, name="stage", tag="stage", bufs=6, align_bytes=64)
 
-        def round_weight(raw, scalar_share):
-            staged = stage_tile()
+        def round_weight(raw, scalar_share, staged=None):
+            if staged is None:
+                staged = stage_tile()
             dst = staged[:].rearrange("p (t c j) -> p c j t", t=PACK, j=PACK)
             src = raw[:].rearrange("p j (c t) -> p c j t", t=PACK)
             if scalar_share > 0:
@@ -176,7 +181,7 @@ def tile_list_pass_tile_scores_kernel(
         def first_stage(b, i):
             for half in range(2):
                 js = slice(BANK * half, BANK * (half + 1))
-                if b == 1:
+                if (b, i, half) not in sums:
                     first_pass(b, i, half, 0)
                 first_pass(b, i, half, 1)
                 nc.vector.tensor_tensor(h[b, i][:, js], sums[b, i, half][:], h[b, i][:, js], ALU.mult)
@@ -202,13 +207,16 @@ def tile_list_pass_tile_scores_kernel(
             for half in range(2):
                 first_pass(0, i, half, 0)
         first_stage(0, 0)
-        staged = round_weight(w1_raw[0, 1], P)
+        staged01 = round_weight(w1_raw[0, 1], 0)
         first_stage(0, 1)
-        w1q[0, 1] = quantize(staged, GROUP, "w1_01")
         first_stage(0, 2)
-        staged = round_weight(w1_raw[1, 1], P)
+        staged11 = round_weight(w1_raw[1, 1], P)
+        w1q[0, 1] = quantize(staged01, GROUP, "w1_01")
+        for i in range(2):
+            for half in range(2):
+                first_pass(1, i, half, 0)
+        w1q[1, 1] = quantize(staged11, GROUP, "w1_11")
         first_stage(0, 3)
-        w1q[1, 1] = quantize(staged, GROUP, "w1_11")
         for i in range(PACK):
             first_stage(1, i)
         for b in range(2):
@@ -245,18 +253,19 @@ def tile_list_pass_tile_scores_kernel(
         def amplitude(g, half):
             ms = slice(HALF * half, HALF * (half + 1))
             s, q = sines[g, half], squares[g, half]
+            accs = [psum.tile([P, 2, HALF], F32, name="bank", tag="bank") for pair in range(2)]
+            for a in range(2):
+                w_codes, w_plane = w3q[a, g]
+                codes, plane = xq[a, half]
+                for t in range(PACK):
+                    cols = slice(P * t, P * (t + 1))
+                    nc.tensor.matmul_mx(
+                        out=accs[t // 2][:, t % 2, :], lhsT=w_codes[:, cols].bitcast(FP8X4), lhsT_scale=w_plane[:, cols],
+                        rhs=codes[:].bitcast(FP8X4), rhs_scale=plane[:],
+                        start=(a == 0 and t % 2 == 0), stop=(a == 1 and t % 2 == 1),
+                    )
             for pair in range(2):
-                acc = psum.tile([P, 2, HALF], F32, name="bank", tag="bank")
-                for k in range(2):
-                    cols = slice(P * (2 * pair + k), P * (2 * pair + k + 1))
-                    for a in range(2):
-                        w_codes, w_plane = w3q[a, g]
-                        codes, plane = xq[a, half]
-                        nc.tensor.matmul_mx(
-                            out=acc[:, k, :], lhsT=w_codes[:, cols].bitcast(FP8X4), lhsT_scale=w_plane[:, cols],
-                            rhs=codes[:].bitcast(FP8X4), rhs_scale=plane[:],
-                            start=(a == 0), stop=(a == 1),
-                        )
+                acc = accs[pair]
                 rows = q[:, 2 * pair : 2 * pair + 2, :]
                 nc.vector.scalar_tensor_tensor(rows, rows, 1.0, acc[:], ALU.subtract, ALU.mult)
             nc.sync.dma_start(dealt_rows(out_0, g)[:, :, ms], q[:])
@@ -274,26 +283,27 @@ def tile_list_pass_tile_scores_kernel(
                 out_1[g].rearrange("p m t -> p (m t)").bitcast(I32)[:, ms], codes[:].bitcast(I32)
             )
 
-        staged = round_weight(w3_raw[0, 0], P)
+        w3q[0, 0] = quantize(round_weight(w3_raw[0, 0], P), GROUP, "w3_00")
         phase(0, 0)
         phase(0, 1)
-        w3q[0, 0] = quantize(staged, GROUP, "w3_00")
-        w3q[1, 0] = quantize(round_weight(w3_raw[1, 0], P), GROUP, "w3_10")
+        staged = round_weight(w3_raw[1, 0], 0)
+        staged01 = round_weight(w3_raw[0, 1], P)
+        w3q[1, 0] = quantize(staged, GROUP, "w3_10")
         phase(1, 0)
-        staged = round_weight(w3_raw[0, 1], P)
         phase(1, 1)
         amplitude(0, 0)
         amplitude(0, 1)
-        w3q[0, 1] = quantize(staged, GROUP, "w3_01")
-        w3q[1, 1] = quantize(round_weight(w3_raw[1, 1], 0), GROUP, "w3_11")
-        planes(0, 0, on_s)
+        staged = round_weight(w3_raw[1, 1], 0)
+        w3q[0, 1] = quantize(staged01, GROUP, "w3_01")
+        w3q[1, 1] = quantize(staged, GROUP, "w3_11")
+        planes(0, 0, on_v)
         planes(0, 1, on_s)
         amplitude(1, 0)
         amplitude(1, 1)
-        planes(1, 0, on_v)
+        planes(1, 0, on_s)
         planes(1, 1, on_v)
         for q in range(4):
-            nc.sync.dma_start(
+            nc.scalar.dma_start(
                 out_2[:, 4 * q : 4 * q + 4, :].bitcast(I32).rearrange("g r m -> r g m"),
                 y_plane[32 * q : 32 * q + 4, :, :].bitcast(I32),
             )

@@ -41,24 +41,17 @@ def tile_list_pass_tile_scores_kernel(
         look_lists = keep.tile([P, M // 16], U16, name="look_lists")
         nc.sync.dma_start(look_lists[:], offs2)
 
-        w2_plane_raw = keep.tile([P, 2 * N], U8, name="w2_plane_raw", align_bytes=64)
-        nc.gpsimd.memset(w2_plane_raw[:].bitcast(I32), 0)
         tab_plane = keep.tile([P, T], U8, name="tab_plane", tag="tab_plane", align_bytes=64)
         nc.vector.memset(tab_plane[:].bitcast(I32), 0)
-        for q in range(4):
-            nc.gpsimd.dma_start(
-                tab_plane[32 * q : 32 * q + 8, :].bitcast(I32),
-                tab_scales[:, 4 * q : 4 * q + 4, :].bitcast(I32),
-            )
         slope_sb = keep.tile([P, 2, PACK], F32, name="slope_sb")
         nc.sync.dma_start(slope_sb[:], slope.rearrange("(b p i) -> p b i", b=2, i=PACK))
         thr_sb = keep.tile([P, 2, PACK], F32, name="thr_sb")
         nc.sync.dma_start(thr_sb[:], thr.rearrange("(b p i) -> p b i", b=2, i=PACK))
+        w2_plane_raw = keep.tile([P, 2 * N], U8, name="w2_plane_raw", align_bytes=64)
+        nc.gpsimd.memset(w2_plane_raw[:].bitcast(I32), 0)
         w2_raw = keep.tile([P, 2 * 2 * N], U8, name="w2_raw", align_bytes=64)
-        nc.sync.dma_start(
-            w2_raw[:].bitcast(I32).rearrange("p (a n) -> p a n", a=2),
-            w2_words.bitcast(I32).rearrange("a p n -> p a n"),
-        )
+        for a in range(2):
+            nc.sync.dma_start(w2_raw[:, 2 * N * a : 2 * N * (a + 1)].bitcast(I32), w2_words[a].bitcast(I32))
 
         def load_table(a, pieces):
             t = keep.tile([P, T], I32, name="table", tag="table", bufs=2, align_bytes=64)
@@ -84,18 +77,23 @@ def tile_list_pass_tile_scores_kernel(
             return t
 
         table, w1_raw, w3_raw, h, plan_sb, z = {}, {}, {}, {}, {}, {}
-        table[0] = load_table(0, 2)
+        table[0] = load_table(0, 1)
         w1_raw[0, 0] = load_weight(w1, 0, 0, "w_raw")
+        for q in range(4):
+            nc.sync.dma_start(
+                tab_plane[32 * q : 32 * q + 8, :].bitcast(I32),
+                tab_scales[:, 4 * q : 4 * q + 4, :].bitcast(I32),
+            )
+        table[1] = load_table(1, 1)
+        w1_raw[1, 0] = load_weight(w1, 1, 0, "w_raw")
+        h[0, 0] = load_sky(0, 0)
+        w1_raw[0, 1] = load_weight(w1, 0, 1, "w_raw")
         for q in range(4):
             nc.sync.dma_start(
                 w2_plane_raw[32 * q : 32 * q + 4, :].bitcast(I32).rearrange("r (a n) -> r a n", a=2),
                 w2_scales[:, 4 * q : 4 * q + 4, :].bitcast(I32).rearrange("a r n -> r a n"),
             )
 
-        table[1] = load_table(1, 1)
-        w1_raw[1, 0] = load_weight(w1, 1, 0, "w_raw")
-        h[0, 0] = load_sky(0, 0)
-        w1_raw[0, 1] = load_weight(w1, 0, 1, "w_raw")
         h[0, 1] = load_sky(0, 1)
         w1_raw[1, 1] = load_weight(w1, 1, 1, "w_raw")
         h[0, 2] = load_sky(0, 2)
@@ -152,11 +150,6 @@ def tile_list_pass_tile_scores_kernel(
         gather_words(0, 1, "v01")
         v_plane = keep.tile([P, S], U8, name="v_plane", align_bytes=64)
         nc.vector.tensor_copy(v_plane[:], tab_plane[:].indirect(pass_list[:]))
-        w2_plane = keep.tile([P, 2 * N], U8, name="w2_plane", align_bytes=64)
-        nc.vector.tensor_copy(
-            w2_plane[:].rearrange("p (u t c) -> p u c t", u=4, t=PACK),
-            w2_plane_raw[:].rearrange("p (u c t) -> p u c t", u=4, t=PACK),
-        )
         w1q[0, 0] = quantize(round_weight(w1_raw[0, 0], P), GROUP, "w1_00")
         gather_words(1, 0, "tab_plane")
         gather_words(1, 1, "v11")
@@ -212,6 +205,11 @@ def tile_list_pass_tile_scores_kernel(
         first_stage(0, 2)
         staged11 = round_weight(w1_raw[1, 1], P)
         w1q[0, 1] = quantize(staged01, GROUP, "w1_01")
+        w2_plane = keep.tile([P, 2 * N], U8, name="w2_plane", align_bytes=64)
+        nc.vector.tensor_copy(
+            w2_plane[:].rearrange("p (u t c) -> p u c t", u=4, t=PACK),
+            w2_plane_raw[:].rearrange("p (u c t) -> p u c t", u=4, t=PACK),
+        )
         for i in range(2):
             for half in range(2):
                 first_pass(1, i, half, 0)

@@ -22,6 +22,7 @@ PACK = 4
 GROUP = P * PACK
 BANK = 512
 HALF = M // 2
+QUADRANTS = 4
 
 
 def tile_list_pass_tile_scores_kernel(
@@ -33,131 +34,134 @@ def tile_list_pass_tile_scores_kernel(
         keep = ctx.enter_context(tc.tile_pool(name="keep", bufs=1))
         psum = ctx.enter_context(tc.psum_pool(name="psum", bufs=8))
 
+        def sb(shape, dtype, tag, bufs=1):
+            return keep.tile(shape, dtype, name=tag, tag=tag, bufs=bufs, align_bytes=64)
+
         def dealt_rows(src, g):
             return src[GROUP * g : GROUP * (g + 1), :].rearrange("(p i) c -> p i c", i=PACK)
+
+        tab_plane = sb([P, T], U8, "tab_plane")
+        nc.vector.memset(tab_plane[:].bitcast(I32), 0)
+        w2_plane_raw = sb([P, 2 * N], U8, "w2_plane_raw")
+        nc.vector.memset(w2_plane_raw[:].bitcast(I32), 0)
 
         pass_list = keep.tile([P, S // 16], U16, name="pass_list")
         nc.sync.dma_start(pass_list[:], offs)
         look_lists = keep.tile([P, M // 16], U16, name="look_lists")
         nc.sync.dma_start(look_lists[:], offs2)
-
-        tab_plane = keep.tile([P, T], U8, name="tab_plane", tag="tab_plane", align_bytes=64)
-        nc.vector.memset(tab_plane[:].bitcast(I32), 0)
-        slope_sb = keep.tile([P, 2, PACK], F32, name="slope_sb")
+        slope_sb = sb([P, 2, PACK], F32, "slope")
         nc.sync.dma_start(slope_sb[:], slope.rearrange("(b p i) -> p b i", b=2, i=PACK))
-        thr_sb = keep.tile([P, 2, PACK], F32, name="thr_sb")
+        thr_sb = sb([P, 2, PACK], F32, "thr")
         nc.sync.dma_start(thr_sb[:], thr.rearrange("(b p i) -> p b i", b=2, i=PACK))
-        w2_plane_raw = keep.tile([P, 2 * N], U8, name="w2_plane_raw", align_bytes=64)
-        nc.gpsimd.memset(w2_plane_raw[:].bitcast(I32), 0)
-        w2_raw = keep.tile([P, 2 * 2 * N], U8, name="w2_raw", align_bytes=64)
+        w2_raw = sb([P, 2 * 2 * N], U8, "w2_raw")
         for a in range(2):
             nc.sync.dma_start(w2_raw[:, 2 * N * a : 2 * N * (a + 1)].bitcast(I32), w2_words[a].bitcast(I32))
 
         def load_table(a, pieces):
-            t = keep.tile([P, T], I32, name="table", tag="table", bufs=2, align_bytes=64)
+            words = sb([P, T], I32, "table", 2)
             src = tab_words[a].rearrange("p n i -> p (n i)").bitcast(I32)
             for u in range(pieces):
                 cols = slice(u * T // pieces, (u + 1) * T // pieces)
-                nc.sync.dma_start(t[:, cols], src[:, cols])
-            return t
+                nc.sync.dma_start(words[:, cols], src[:, cols])
+            return words
 
-        def load_weight(w, a, g, tag):
-            t = keep.tile([P, PACK, GROUP], F32, name=tag, tag=tag, bufs=6, align_bytes=64)
-            nc.sync.dma_start(t[:], dealt_rows(w, a)[:, :, GROUP * g : GROUP * (g + 1)])
-            return t
+        def load_table_scales(a):
+            for q in range(QUADRANTS):
+                nc.sync.dma_start(
+                    tab_plane[32 * q + 4 * a : 32 * q + 4 * a + 4, :].bitcast(I32),
+                    tab_scales[a, 4 * q : 4 * q + 4, :].bitcast(I32),
+                )
+
+        def load_w2_scales():
+            for q in range(QUADRANTS):
+                nc.sync.dma_start(
+                    w2_plane_raw[32 * q : 32 * q + 4, :].bitcast(I32).rearrange("r (a n) -> r a n", a=2),
+                    w2_scales[:, 4 * q : 4 * q + 4, :].bitcast(I32).rearrange("a r n -> r a n"),
+                )
+
+        def load_weight(w, a, g, tag="w_raw", bufs=6):
+            raw = sb([P, PACK, GROUP], F32, tag, bufs)
+            nc.sync.dma_start(raw[:], dealt_rows(w, a)[:, :, GROUP * g : GROUP * (g + 1)])
+            return raw
 
         def load_sky(b, i):
-            t = keep.tile([P, S], F32, name="rows", tag="rows", bufs=8, align_bytes=64)
-            nc.sync.dma_start(t[:], dealt_rows(sky, b)[:, i, :])
-            return t
+            rows = sb([P, S], F32, "rows", 8)
+            nc.sync.dma_start(rows[:], dealt_rows(sky, b)[:, i, :])
+            return rows
 
         def load_matrix(src, g, tag):
-            t = keep.tile([P, PACK, M], F32, name=tag, tag=tag, bufs=2, align_bytes=64)
-            nc.sync.dma_start(t[:], dealt_rows(src, g))
-            return t
+            rows = sb([P, PACK, M], F32, tag, 2)
+            nc.sync.dma_start(rows[:], dealt_rows(src, g))
+            return rows
 
-        table, w1_raw, w3_raw, h, plan_sb, z = {}, {}, {}, {}, {}, {}
-        table[0] = load_table(0, 1)
-        w1_raw[0, 0] = load_weight(w1, 0, 0, "w_raw")
-        for q in range(4):
-            nc.sync.dma_start(
-                tab_plane[32 * q : 32 * q + 8, :].bitcast(I32),
-                tab_scales[:, 4 * q : 4 * q + 4, :].bitcast(I32),
-            )
+        table, w1_raw, w3_raw, h, plan_sb, weather_sb = {}, {}, {}, {}, {}, {}
+        table[0] = load_table(0, 2)
+        load_table_scales(0)
+        w1_raw[0, 0] = load_weight(w1, 0, 0)
+        w1_raw[1, 0] = load_weight(w1, 1, 0)
+        load_table_scales(1)
         table[1] = load_table(1, 1)
-        w1_raw[1, 0] = load_weight(w1, 1, 0, "w_raw")
         h[0, 0] = load_sky(0, 0)
-        w1_raw[0, 1] = load_weight(w1, 0, 1, "w_raw")
-        for q in range(4):
-            nc.sync.dma_start(
-                w2_plane_raw[32 * q : 32 * q + 4, :].bitcast(I32).rearrange("r (a n) -> r a n", a=2),
-                w2_scales[:, 4 * q : 4 * q + 4, :].bitcast(I32).rearrange("a r n -> r a n"),
-            )
-
+        w1_raw[0, 1] = load_weight(w1, 0, 1)
+        load_w2_scales()
+        w1_raw[1, 1] = load_weight(w1, 1, 1)
         h[0, 1] = load_sky(0, 1)
-        w1_raw[1, 1] = load_weight(w1, 1, 1, "w_raw")
         h[0, 2] = load_sky(0, 2)
         h[0, 3] = load_sky(0, 3)
         h[1, 0] = load_sky(1, 0)
         h[1, 1] = load_sky(1, 1)
         h[1, 2] = load_sky(1, 2)
         h[1, 3] = load_sky(1, 3)
-        plan_sb[0] = load_matrix(plan, 0, "plan_sb")
-        plan_sb[1] = load_matrix(plan, 1, "plan_sb")
-        w3_raw[0, 0] = load_weight(w3, 0, 0, "w_raw")
-        z[0] = load_matrix(weather, 0, "z")
-        w3_raw[1, 0] = load_weight(w3, 1, 0, "w_raw")
-        z[1] = load_matrix(weather, 1, "z")
-        w3_raw[0, 1] = load_weight(w3, 0, 1, "w_raw")
-        w3_raw[1, 1] = load_weight(w3, 1, 1, "w_raw")
+        plan_sb[0] = load_matrix(plan, 0, "plan")
+        plan_sb[1] = load_matrix(plan, 1, "plan")
+        w3_raw[0, 0] = load_weight(w3, 0, 0)
+        weather_sb[0] = load_matrix(weather, 0, "weather")
+        w3_raw[1, 0] = load_weight(w3, 1, 0, "w3_10_raw", 1)
+        weather_sb[1] = load_matrix(weather, 1, "weather")
+        w3_raw[0, 1] = load_weight(w3, 0, 1)
+        w3_raw[1, 1] = load_weight(w3, 1, 1)
 
-        w2_codes = keep.tile([P, 2 * 2 * N], U8, name="w2_codes", align_bytes=64)
+        def round_weight(raw, copy, staged):
+            dst = staged[:].rearrange("p (t c j) -> p c j t", t=PACK, j=PACK)
+            src = raw[:].rearrange("p j (c t) -> p c j t", t=PACK)
+            for t in range(0, PACK, 2):
+                copy(dst[:, :, :, t : t + 2], src[:, :, :, t : t + 2])
+            return staged
+
+        def quantize(staged, width, tag):
+            codes = sb([P, width], U32, tag + "_codes")
+            plane = sb([P, width], U8, tag + "_plane")
+            nc.vector.quantize_mx(out=codes[:].bitcast(FP8X4), scales=plane[:], in_=staged[:])
+            return codes, plane
+
+        def wide(tag, bufs=1):
+            return sb([P, PACK * GROUP], BF16, tag, bufs)
+
+        def gather_words(a, tag):
+            codes = sb([P, S], U32, tag)
+            for half in range(2):
+                entries = pass_list[:, 32 * half : 32 * (half + 1)]
+                nc.vector.tensor_copy(
+                    codes[:, BANK * half : BANK * (half + 1)], table[a][:].bitcast(U32).indirect(entries)
+                )
+            return codes
+
+        on_scalar, on_vector = nc.scalar.copy, nc.vector.tensor_copy
+        w1q, w3q, xq, v_codes = {}, {}, {}, {}
+
+        w2_codes = sb([P, 2 * 2 * N], U8, "w2_codes")
         nc.vector.tensor_copy(
             w2_codes[:].rearrange("p (u t c e) -> p u c t e", u=4, t=PACK, e=2),
             w2_raw[:].rearrange("p (u c t e) -> p u c t e", u=4, t=PACK, e=2),
         )
-
-        v_codes = {}
-
-        def gather_words(a, half, tag):
-            entries = pass_list[:, 32 * half : 32 * (half + 1)]
-            v_codes[a, half] = keep.tile([P, BANK], U32, name=tag, tag=tag, align_bytes=64)
-            nc.vector.tensor_copy(v_codes[a, half][:], table[a][:].bitcast(U32).indirect(entries))
-
-        def stage_tile():
-            return keep.tile([P, PACK * GROUP], BF16, name="stage", tag="stage", bufs=6, align_bytes=64)
-
-        def round_weight(raw, scalar_share, staged=None):
-            if staged is None:
-                staged = stage_tile()
-            dst = staged[:].rearrange("p (t c j) -> p c j t", t=PACK, j=PACK)
-            src = raw[:].rearrange("p j (c t) -> p c j t", t=PACK)
-            if scalar_share > 0:
-                nc.scalar.copy(dst[:, :scalar_share], src[:, :scalar_share])
-            if scalar_share < P:
-                nc.vector.tensor_copy(dst[:, scalar_share:], src[:, scalar_share:])
-            return staged
-
-        def quantize(staged, width, name):
-            codes = keep.tile([P, width], U32, name=name + "_codes", align_bytes=64)
-            plane = keep.tile([P, width], U8, name=name + "_plane", align_bytes=64)
-            nc.vector.quantize_mx(out=codes[:].bitcast(FP8X4), scales=plane[:], in_=staged[:, : PACK * width])
-            return codes, plane
-
-        w1q, w3q, xq = {}, {}, {}
-        on_s, on_v = nc.scalar.copy, nc.vector.tensor_copy
-        gather_words(0, 0, "v00")
-        gather_words(0, 1, "v01")
-        v_plane = keep.tile([P, S], U8, name="v_plane", align_bytes=64)
+        v_codes[0] = gather_words(0, "v0")
+        v_plane = sb([P, S], U8, "v_plane")
         nc.vector.tensor_copy(v_plane[:], tab_plane[:].indirect(pass_list[:]))
-        w1q[0, 0] = quantize(round_weight(w1_raw[0, 0], P), GROUP, "w1_00")
-        gather_words(1, 0, "tab_plane")
-        gather_words(1, 1, "v11")
-        w1q[1, 0] = quantize(round_weight(w1_raw[1, 0], 48), GROUP, "w1_10")
+        w1q[0, 0] = quantize(round_weight(w1_raw[0, 0], on_scalar, wide("w1_00_staged")), GROUP, "w1_00")
+        w1q[1, 0] = quantize(round_weight(w1_raw[1, 0], on_scalar, wide("v1")), GROUP, "w1_10")
+        v_codes[1] = gather_words(1, "v1")
 
-        looks = {}
-
-        sums = {}
+        looks, sums = {}, {}
 
         def first_pass(b, i, half, a):
             cols = slice(P * i, P * (i + 1))
@@ -167,141 +171,141 @@ def tile_list_pass_tile_scores_kernel(
             codes, plane = w1q[a, b]
             nc.tensor.matmul_mx(
                 out=sums[b, i, half][:], lhsT=codes[:, cols].bitcast(FP8X4), lhsT_scale=plane[:, cols],
-                rhs=v_codes[a, half][:].bitcast(FP8X4), rhs_scale=v_plane[4 * a :, js],
+                rhs=v_codes[a][:, js].bitcast(FP8X4), rhs_scale=v_plane[4 * a :, js],
                 start=(a == 0), stop=(a == 1),
             )
 
-        def first_stage(b, i):
+        def open_sums(b, rows):
+            for i in rows:
+                for half in range(2):
+                    first_pass(b, i, half, 0)
+
+        def look(b, i):
             for half in range(2):
                 js = slice(BANK * half, BANK * (half + 1))
-                if (b, i, half) not in sums:
-                    first_pass(b, i, half, 0)
                 first_pass(b, i, half, 1)
                 nc.vector.tensor_tensor(h[b, i][:, js], sums[b, i, half][:], h[b, i][:, js], ALU.mult)
             if i == 0:
-                looks[b] = keep.tile([P, PACK, M], F32, name="looks", tag="table", bufs=2, align_bytes=64)
+                looks[b] = sb([P, PACK, M], F32, "table", 2)
             nc.scalar.activation(
                 out=looks[b][:, i, :], in_=h[b, i][:].indirect(look_lists[:]), func=ACT.Sigmoid,
                 bias=thr_sb[:, b, i : i + 1], scale=slope_sb[:, b, i : i + 1],
             )
 
-        def make_x(b, half):
+        def make_x(b, half, tag):
             ms = slice(HALF * half, HALF * (half + 1))
-            staged = stage_tile()
+            staged = sb([P, PACK * HALF], BF16, tag)
             nc.vector.tensor_tensor(
-                staged[:, : PACK * HALF].rearrange("p (c k i) -> p c i k", i=PACK, k=4),
+                staged[:].rearrange("p (c k i) -> p c i k", i=PACK, k=4),
                 looks[b][:, :, ms].rearrange("p i (c k) -> p c i k", k=4),
                 plan_sb[b][:, :, ms].rearrange("p i (c k) -> p c i k", k=4),
                 ALU.mult,
             )
             return staged
 
-        for i in range(PACK):
-            for half in range(2):
-                first_pass(0, i, half, 0)
-        first_stage(0, 0)
-        staged01 = round_weight(w1_raw[0, 1], 0)
-        first_stage(0, 1)
-        first_stage(0, 2)
-        staged11 = round_weight(w1_raw[1, 1], P)
-        w1q[0, 1] = quantize(staged01, GROUP, "w1_01")
-        w2_plane = keep.tile([P, 2 * N], U8, name="w2_plane", align_bytes=64)
+        open_sums(0, range(PACK))
+        look(0, 0)
+        w1q[0, 1] = quantize(round_weight(w1_raw[0, 1], on_vector, wide("w1_00_staged")), GROUP, "w1_01")
+        w2_plane = sb([P, 2 * N], U8, "w2_plane")
         nc.vector.tensor_copy(
             w2_plane[:].rearrange("p (u t c) -> p u c t", u=4, t=PACK),
             w2_plane_raw[:].rearrange("p (u c t) -> p u c t", u=4, t=PACK),
         )
-        for i in range(2):
-            for half in range(2):
-                first_pass(1, i, half, 0)
-        w1q[1, 1] = quantize(staged11, GROUP, "w1_11")
-        first_stage(0, 3)
-        for i in range(PACK):
-            first_stage(1, i)
+        staged = round_weight(w1_raw[1, 1], on_scalar, wide("rows", 8))
+        look(0, 1)
+        look(0, 2)
+        open_sums(1, range(2))
+        w1q[1, 1] = quantize(staged, GROUP, "w1_11")
+        look(0, 3)
+        look(1, 0)
+        open_sums(1, range(2, PACK))
+        for i in range(1, PACK):
+            look(1, i)
+        staged_w3 = round_weight(w3_raw[0, 0], on_scalar, wide("slope"))
         for b in range(2):
-            staged = [make_x(b, half) for half in range(2)]
+            staged = [make_x(b, half, ("w1_11_codes", "v1", "x10", "x11")[2 * b + half]) for half in range(2)]
             for half in range(2):
                 xq[b, half] = quantize(staged[half], HALF, f"x_{b}{half}")
 
-        y_plane = keep.tile([P, 2, M], U8, name="y_plane", align_bytes=64)
-        sines, squares = {}, {}
+        y_plane = sb([P, 2, M], U8, "y_plane")
+        y = {}
 
-        def phase(g, half):
-            ms = slice(HALF * half, HALF * (half + 1))
-            for pair in range(2):
-                acc = psum.tile([P, 2, HALF], F32, name="bank", tag="bank")
-                for k in range(2):
-                    t = 2 * pair + k
-                    for a in range(2):
-                        col = N * a + GROUP * g + P * t
-                        codes, plane = xq[a, half]
-                        nc.tensor.matmul_mx(
-                            out=acc[:, k, :], lhsT=w2_codes[:, 2 * col : 2 * (col + P)].bitcast(FP4X4),
-                            lhsT_scale=w2_plane[:, col : col + P],
-                            rhs=codes[:].bitcast(FP8X4), rhs_scale=plane[:],
-                            start=(a == 0), stop=(a == 1),
-                        )
-                rows = z[g][:, 2 * pair : 2 * pair + 2, ms]
-                nc.vector.scalar_tensor_tensor(rows, acc[:], math.pi / 2, rows, ALU.add, ALU.add)
-            s = keep.tile([P, PACK, HALF], F32, name="sines", tag="rows", bufs=8, align_bytes=64)
-            nc.scalar.activation(out=s[:], in_=z[g][:, :, ms], func=ACT.Sin, scale=0.5)
-            q = keep.tile([P, PACK, HALF], F32, name="squares", tag="rows", bufs=8, align_bytes=64)
-            nc.scalar.activation(out=q[:], in_=s[:], func=ACT.Square, scale=math.sqrt(2.0))
-            sines[g, half], squares[g, half] = s, q
-
-        def amplitude(g, half):
-            ms = slice(HALF * half, HALF * (half + 1))
-            s, q = sines[g, half], squares[g, half]
+        def second_sums(half, stationary):
             accs = [psum.tile([P, 2, HALF], F32, name="bank", tag="bank") for pair in range(2)]
             for a in range(2):
-                w_codes, w_plane = w3q[a, g]
                 codes, plane = xq[a, half]
                 for t in range(PACK):
-                    cols = slice(P * t, P * (t + 1))
+                    w_codes, w_plane = stationary(a, t)
                     nc.tensor.matmul_mx(
-                        out=accs[t // 2][:, t % 2, :], lhsT=w_codes[:, cols].bitcast(FP8X4), lhsT_scale=w_plane[:, cols],
+                        out=accs[t // 2][:, t % 2, :], lhsT=w_codes, lhsT_scale=w_plane,
                         rhs=codes[:].bitcast(FP8X4), rhs_scale=plane[:],
                         start=(a == 0 and t % 2 == 0), stop=(a == 1 and t % 2 == 1),
                     )
+            return accs
+
+        def phase(g, half, angle):
+            ms = slice(HALF * half, HALF * (half + 1))
+
+            def w2_columns(a, t):
+                col = N * a + GROUP * g + P * t
+                return w2_codes[:, 2 * col : 2 * (col + P)].bitcast(FP4X4), w2_plane[:, col : col + P]
+
+            accs = second_sums(half, w2_columns)
             for pair in range(2):
-                acc = accs[pair]
-                rows = q[:, 2 * pair : 2 * pair + 2, :]
-                nc.vector.scalar_tensor_tensor(rows, rows, 1.0, acc[:], ALU.subtract, ALU.mult)
-            nc.sync.dma_start(dealt_rows(out_0, g)[:, :, ms], q[:])
+                ts = slice(2 * pair, 2 * pair + 2)
+                nc.vector.scalar_tensor_tensor(
+                    angle[:, ts, :], accs[pair][:], math.pi / 2, weather_sb[g][:, ts, ms], ALU.add, ALU.add
+                )
+            y[g, half] = sb([P, PACK, HALF], F32, "rows", 8)
+            nc.scalar.activation(out=y[g, half][:], in_=angle[:, :, :], func=ACT.Sin, scale=0.5)
+            nc.scalar.activation(out=y[g, half][:], in_=y[g, half][:], func=ACT.Square, scale=math.sqrt(2.0))
+
+        def amplitude(g, half):
+            ms = slice(HALF * half, HALF * (half + 1))
+
+            def w3_columns(a, t):
+                codes, plane = w3q[a, g]
+                return codes[:, P * t : P * (t + 1)].bitcast(FP8X4), plane[:, P * t : P * (t + 1)]
+
+            accs = second_sums(half, w3_columns)
+            for pair in range(2):
+                rows = y[g, half][:, 2 * pair : 2 * pair + 2, :]
+                nc.vector.scalar_tensor_tensor(rows, rows, 1.0, accs[pair][:], ALU.subtract, ALU.mult)
+            nc.sync.dma_start(dealt_rows(out_0, g)[:, :, ms], y[g, half][:])
 
         def planes(g, half, copy):
             ms = slice(HALF * half, HALF * (half + 1))
-            staged = stage_tile()
+            staged = sb([P, PACK * HALF], BF16, "y_staged", 2)
             copy(
-                staged[:, : PACK * HALF].rearrange("p (c k t) -> p c t k", t=PACK, k=4),
-                squares[g, half][:].rearrange("p t (c k) -> p c t k", k=4),
+                staged[:].rearrange("p (c k t) -> p c t k", t=PACK, k=4),
+                y[g, half][:].rearrange("p t (c k) -> p c t k", k=4),
             )
-            codes = keep.tile([P, HALF], U32, name=f"y_codes{g}{half}", align_bytes=64)
-            nc.vector.quantize_mx(out=codes[:].bitcast(FP8X4), scales=y_plane[:, g, ms], in_=staged[:, : PACK * HALF])
-            nc.sync.dma_start(
-                out_1[g].rearrange("p m t -> p (m t)").bitcast(I32)[:, ms], codes[:].bitcast(I32)
-            )
+            codes = sb([P, HALF], U32, "y_codes", 4)
+            nc.vector.quantize_mx(out=codes[:].bitcast(FP8X4), scales=y_plane[:, g, ms], in_=staged[:])
+            nc.sync.dma_start(out_1[g].rearrange("p m t -> p (m t)").bitcast(I32)[:, ms], codes[:].bitcast(I32))
 
-        w3q[0, 0] = quantize(round_weight(w3_raw[0, 0], P), GROUP, "w3_00")
-        phase(0, 0)
-        phase(0, 1)
-        staged = round_weight(w3_raw[1, 0], 0)
-        staged01 = round_weight(w3_raw[0, 1], P)
+        w3q[0, 0] = quantize(staged_w3, GROUP, "w3_00")
+        phase(0, 0, sb([P, PACK, HALF], F32, "rows", 8))
+        phase(0, 1, sb([P, PACK, HALF], F32, "angle01"))
+        staged = round_weight(w3_raw[1, 0], on_vector, wide("weather", 2))
+        staged_w3 = round_weight(w3_raw[0, 1], on_scalar, wide("angle01"))
         w3q[1, 0] = quantize(staged, GROUP, "w3_10")
-        phase(1, 0)
-        phase(1, 1)
+        angles = sb([P, 2, PACK, HALF], F32, "w3_10_raw")
+        phase(1, 0, angles[:, 0])
+        phase(1, 1, angles[:, 1])
         amplitude(0, 0)
         amplitude(0, 1)
-        staged = round_weight(w3_raw[1, 1], 0)
-        w3q[0, 1] = quantize(staged01, GROUP, "w3_01")
+        staged = round_weight(w3_raw[1, 1], on_vector, wide("weather", 2))
+        w3q[0, 1] = quantize(staged_w3, GROUP, "w3_01")
         w3q[1, 1] = quantize(staged, GROUP, "w3_11")
-        planes(0, 0, on_v)
-        planes(0, 1, on_s)
+        planes(0, 0, on_vector)
+        planes(0, 1, on_scalar)
         amplitude(1, 0)
         amplitude(1, 1)
-        planes(1, 0, on_s)
-        planes(1, 1, on_v)
-        for q in range(4):
-            nc.scalar.dma_start(
+        planes(1, 0, on_scalar)
+        planes(1, 1, on_vector)
+        for q in range(QUADRANTS):
+            (nc.scalar if q % 2 else nc.sync).dma_start(
                 out_2[:, 4 * q : 4 * q + 4, :].bitcast(I32).rearrange("g r m -> r g m"),
                 y_plane[32 * q : 32 * q + 4, :, :].bitcast(I32),
             )

@@ -20,9 +20,15 @@ ACT = mybir.ActivationFunctionType
 P = 128
 PACK = 4
 GROUP = P * PACK
+GROUPS = 2
 BANK = 512
 HALF = M // 2
 QUADRANTS = 4
+BLOCKS = 4
+LIST_ROWS = 16
+LINE = 4
+RAW_BUFS = 6
+STAGE_BUFS = 6
 
 
 def tile_list_pass_tile_scores_kernel(
@@ -34,31 +40,38 @@ def tile_list_pass_tile_scores_kernel(
         keep = ctx.enter_context(tc.tile_pool(name="keep", bufs=1))
         psum = ctx.enter_context(tc.psum_pool(name="psum", bufs=8))
 
-        def sb(shape, dtype, tag, bufs=1):
+        def sbuf(shape, dtype, tag, bufs=1):
             return keep.tile(shape, dtype, name=tag, tag=tag, bufs=bufs, align_bytes=64)
 
-        def dealt_rows(src, g):
-            return src[GROUP * g : GROUP * (g + 1), :].rearrange("(p i) c -> p i c", i=PACK)
+        def by_word(matrix, g):
+            return matrix[GROUP * g : GROUP * (g + 1), :].rearrange("(p t) c -> p t c", t=PACK)
 
-        tab_plane = sb([P, T], U8, "tab_plane")
-        nc.vector.memset(tab_plane[:].bitcast(I32), 0)
-        w2_plane_raw = sb([P, 2 * N], U8, "w2_plane_raw")
-        nc.vector.memset(w2_plane_raw[:].bitcast(I32), 0)
+        def live_rows(plane, quadrant, start=0):
+            return plane[32 * quadrant + start : 32 * quadrant + start + BLOCKS]
 
-        pass_list = keep.tile([P, S // 16], U16, name="pass_list")
+        def scale_rows(quadrant):
+            return slice(BLOCKS * quadrant, BLOCKS * (quadrant + 1))
+
+        pass_list = keep.tile([P, S // LIST_ROWS], U16, name="pass_list")
         nc.sync.dma_start(pass_list[:], offs)
-        look_lists = keep.tile([P, M // 16], U16, name="look_lists")
+        look_lists = keep.tile([P, M // LIST_ROWS], U16, name="look_lists")
         nc.sync.dma_start(look_lists[:], offs2)
-        slope_sb = sb([P, 2, PACK], F32, "slope")
-        nc.sync.dma_start(slope_sb[:], slope.rearrange("(b p i) -> p b i", b=2, i=PACK))
-        thr_sb = sb([P, 2, PACK], F32, "thr")
-        nc.sync.dma_start(thr_sb[:], thr.rearrange("(b p i) -> p b i", b=2, i=PACK))
-        w2_raw = sb([P, 2 * 2 * N], U8, "w2_raw")
-        for a in range(2):
+
+        tab_plane = sbuf([P, T], U8, "tab_plane")
+        nc.vector.memset(tab_plane[:].bitcast(I32), 0)
+        slope_sb = keep.tile([P, GROUPS, PACK], F32, name="slope_sb")
+        nc.sync.dma_start(slope_sb[:], slope.rearrange("(b p t) -> p b t", b=GROUPS, t=PACK))
+        thr_sb = keep.tile([P, GROUPS, PACK], F32, name="thr_sb")
+        nc.sync.dma_start(thr_sb[:], thr.rearrange("(b p t) -> p b t", b=GROUPS, t=PACK))
+        w2_plane_raw = sbuf([P, GROUPS * N], U8, "w2_plane_raw")
+        nc.gpsimd.memset(w2_plane_raw[:].bitcast(I32), 0)
+
+        w2_raw = sbuf([P, GROUPS * 2 * N], U8, "w2_raw")
+        for a in range(GROUPS):
             nc.sync.dma_start(w2_raw[:, 2 * N * a : 2 * N * (a + 1)].bitcast(I32), w2_words[a].bitcast(I32))
 
         def load_table(a, pieces):
-            words = sb([P, T], I32, "table", 2)
+            words = sbuf([P, T], I32, "table", GROUPS)
             src = tab_words[a].rearrange("p n i -> p (n i)").bitcast(I32)
             for u in range(pieces):
                 cols = slice(u * T // pieces, (u + 1) * T // pieces)
@@ -66,246 +79,265 @@ def tile_list_pass_tile_scores_kernel(
             return words
 
         def load_table_scales(a):
-            for q in range(QUADRANTS):
+            for quadrant in range(QUADRANTS):
                 nc.sync.dma_start(
-                    tab_plane[32 * q + 4 * a : 32 * q + 4 * a + 4, :].bitcast(I32),
-                    tab_scales[a, 4 * q : 4 * q + 4, :].bitcast(I32),
+                    live_rows(tab_plane, quadrant, BLOCKS * a).bitcast(I32),
+                    tab_scales[a, scale_rows(quadrant), :].bitcast(I32),
                 )
 
         def load_w2_scales():
-            for q in range(QUADRANTS):
+            for quadrant in range(QUADRANTS):
                 nc.sync.dma_start(
-                    w2_plane_raw[32 * q : 32 * q + 4, :].bitcast(I32).rearrange("r (a n) -> r a n", a=2),
-                    w2_scales[:, 4 * q : 4 * q + 4, :].bitcast(I32).rearrange("a r n -> r a n"),
+                    live_rows(w2_plane_raw, quadrant).bitcast(I32).rearrange("r (a n) -> r a n", a=GROUPS),
+                    w2_scales[:, scale_rows(quadrant), :].bitcast(I32).rearrange("a r n -> r a n"),
                 )
 
-        def load_weight(w, a, g, tag="w_raw", bufs=6):
-            raw = sb([P, PACK, GROUP], F32, tag, bufs)
-            nc.sync.dma_start(raw[:], dealt_rows(w, a)[:, :, GROUP * g : GROUP * (g + 1)])
+        def load_weight(w, a, g):
+            raw = sbuf([P, PACK, GROUP], F32, "w_raw", RAW_BUFS)
+            nc.sync.dma_start(raw[:], by_word(w, a)[:, :, GROUP * g : GROUP * (g + 1)])
             return raw
 
-        def load_sky(b, i):
-            rows = sb([P, S], F32, "rows", 8)
-            nc.sync.dma_start(rows[:], dealt_rows(sky, b)[:, i, :])
+        def row_tile():
+            return sbuf([P, S], F32, "rows", GROUPS * PACK)
+
+        def load_sky(b, t):
+            rows = row_tile()
+            nc.sync.dma_start(rows[:], by_word(sky, b)[:, t, :])
             return rows
 
-        def load_matrix(src, g, tag):
-            rows = sb([P, PACK, M], F32, tag, 2)
-            nc.sync.dma_start(rows[:], dealt_rows(src, g))
+        def load_group(matrix, g, tag):
+            rows = sbuf([P, PACK, M], F32, tag, GROUPS)
+            nc.sync.dma_start(rows[:], by_word(matrix, g))
             return rows
 
-        table, w1_raw, w3_raw, h, plan_sb, weather_sb = {}, {}, {}, {}, {}, {}
+        table, w1_raw, w3_raw, h, plan_sb, angle = {}, {}, {}, {}, {}, {}
         table[0] = load_table(0, 2)
         load_table_scales(0)
         w1_raw[0, 0] = load_weight(w1, 0, 0)
-        w1_raw[1, 0] = load_weight(w1, 1, 0)
         load_table_scales(1)
+        w1_raw[1, 0] = load_weight(w1, 1, 0)
         table[1] = load_table(1, 1)
         h[0, 0] = load_sky(0, 0)
+        h[0, 1] = load_sky(0, 1)
         w1_raw[0, 1] = load_weight(w1, 0, 1)
         load_w2_scales()
         w1_raw[1, 1] = load_weight(w1, 1, 1)
-        h[0, 1] = load_sky(0, 1)
         h[0, 2] = load_sky(0, 2)
         h[0, 3] = load_sky(0, 3)
-        h[1, 0] = load_sky(1, 0)
-        h[1, 1] = load_sky(1, 1)
-        h[1, 2] = load_sky(1, 2)
-        h[1, 3] = load_sky(1, 3)
-        plan_sb[0] = load_matrix(plan, 0, "plan")
-        plan_sb[1] = load_matrix(plan, 1, "plan")
+        for t in range(PACK):
+            h[1, t] = load_sky(1, t)
+        for b in range(GROUPS):
+            plan_sb[b] = load_group(plan, b, "plan")
         w3_raw[0, 0] = load_weight(w3, 0, 0)
-        weather_sb[0] = load_matrix(weather, 0, "weather")
-        w3_raw[1, 0] = load_weight(w3, 1, 0, "w3_10_raw", 1)
-        weather_sb[1] = load_matrix(weather, 1, "weather")
+        angle[0] = load_group(weather, 0, "angle")
+        w3_raw[1, 0] = load_weight(w3, 1, 0)
+        angle[1] = load_group(weather, 1, "angle")
         w3_raw[0, 1] = load_weight(w3, 0, 1)
         w3_raw[1, 1] = load_weight(w3, 1, 1)
 
-        def round_weight(raw, copy, staged):
-            dst = staged[:].rearrange("p (t c j) -> p c j t", t=PACK, j=PACK)
-            src = raw[:].rearrange("p j (c t) -> p c j t", t=PACK)
-            for t in range(0, PACK, 2):
-                copy(dst[:, :, :, t : t + 2], src[:, :, :, t : t + 2])
+        on_scalar, on_vector = nc.scalar.copy, nc.vector.tensor_copy
+
+        def stage_tile():
+            return sbuf([P, PACK * GROUP], BF16, "stage", STAGE_BUFS)
+
+        def round_weight(raw, copy):
+            staged = stage_tile()
+            copy(
+                staged[:].rearrange("p (t c j) -> p c j t", t=PACK, j=PACK),
+                raw[:].rearrange("p j (c t) -> p c j t", t=PACK),
+            )
             return staged
 
         def quantize(staged, width, tag):
-            codes = sb([P, width], U32, tag + "_codes")
-            plane = sb([P, width], U8, tag + "_plane")
-            nc.vector.quantize_mx(out=codes[:].bitcast(FP8X4), scales=plane[:], in_=staged[:])
+            codes = sbuf([P, width], U32, tag + "_codes")
+            plane = sbuf([P, width], U8, tag + "_plane")
+            nc.vector.quantize_mx(out=codes[:].bitcast(FP8X4), scales=plane[:], in_=staged[:, : PACK * width])
             return codes, plane
 
-        def wide(tag, bufs=1):
-            return sb([P, PACK * GROUP], BF16, tag, bufs)
-
-        def gather_words(a, tag):
-            codes = sb([P, S], U32, tag)
-            for half in range(2):
-                entries = pass_list[:, 32 * half : 32 * (half + 1)]
-                nc.vector.tensor_copy(
-                    codes[:, BANK * half : BANK * (half + 1)], table[a][:].bitcast(U32).indirect(entries)
-                )
+        def gather_words(a, part):
+            entries = pass_list[:, part * BANK // LIST_ROWS : (part + 1) * BANK // LIST_ROWS]
+            codes = sbuf([P, BANK], U32, f"v{a}{part}")
+            nc.vector.tensor_copy(codes[:], table[a][:].bitcast(U32).indirect(entries))
             return codes
 
-        on_scalar, on_vector = nc.scalar.copy, nc.vector.tensor_copy
-        w1q, w3q, xq, v_codes = {}, {}, {}, {}
-
-        w2_codes = sb([P, 2 * 2 * N], U8, "w2_codes")
+        w2_codes = sbuf([P, GROUPS * 2 * N], U8, "w2_codes")
         nc.vector.tensor_copy(
-            w2_codes[:].rearrange("p (u t c e) -> p u c t e", u=4, t=PACK, e=2),
-            w2_raw[:].rearrange("p (u c t e) -> p u c t e", u=4, t=PACK, e=2),
+            w2_codes[:].rearrange("p (u t c e) -> p u c t e", u=GROUPS * GROUPS, t=PACK, e=2),
+            w2_raw[:].rearrange("p (u c t e) -> p u c t e", u=GROUPS * GROUPS, t=PACK, e=2),
         )
-        v_codes[0] = gather_words(0, "v0")
-        v_plane = sb([P, S], U8, "v_plane")
+
+        parts = range(S // BANK)
+        w1q, w3q, xq, v_codes = {}, {}, {}, {}
+        for part in parts:
+            v_codes[0, part] = gather_words(0, part)
+        v_plane = sbuf([P, S], U8, "v_plane")
         nc.vector.tensor_copy(v_plane[:], tab_plane[:].indirect(pass_list[:]))
-        w1q[0, 0] = quantize(round_weight(w1_raw[0, 0], on_scalar, wide("w1_00_staged")), GROUP, "w1_00")
-        w1q[1, 0] = quantize(round_weight(w1_raw[1, 0], on_scalar, wide("v1")), GROUP, "w1_10")
-        v_codes[1] = gather_words(1, "v1")
+        for a in range(GROUPS):
+            w1q[a, 0] = quantize(round_weight(w1_raw[a, 0], on_scalar), GROUP, f"w1_{a}0")
+        for part in parts:
+            v_codes[1, part] = gather_words(1, part)
 
-        looks, sums = {}, {}
+        sums, looks = {}, {}
 
-        def first_pass(b, i, half, a):
-            cols = slice(P * i, P * (i + 1))
-            js = slice(BANK * half, BANK * (half + 1))
+        def first_pass(b, t, part, a):
+            cols = slice(P * t, P * (t + 1))
             if a == 0:
-                sums[b, i, half] = psum.tile([P, BANK], F32, name="bank", tag="bank")
+                sums[b, t, part] = psum.tile([P, BANK], F32, name="bank", tag="bank")
             codes, plane = w1q[a, b]
             nc.tensor.matmul_mx(
-                out=sums[b, i, half][:], lhsT=codes[:, cols].bitcast(FP8X4), lhsT_scale=plane[:, cols],
-                rhs=v_codes[a][:, js].bitcast(FP8X4), rhs_scale=v_plane[4 * a :, js],
-                start=(a == 0), stop=(a == 1),
+                out=sums[b, t, part][:],
+                lhsT=codes[:, cols].bitcast(FP8X4),
+                lhsT_scale=plane[:, cols],
+                rhs=v_codes[a, part][:].bitcast(FP8X4),
+                rhs_scale=v_plane[BLOCKS * a :, BANK * part : BANK * (part + 1)],
+                start=(a == 0),
+                stop=(a == GROUPS - 1),
             )
 
-        def open_sums(b, rows):
-            for i in rows:
-                for half in range(2):
-                    first_pass(b, i, half, 0)
+        def open_sums(b, slices):
+            for t in slices:
+                for part in parts:
+                    first_pass(b, t, part, 0)
 
-        def look(b, i):
-            for half in range(2):
-                js = slice(BANK * half, BANK * (half + 1))
-                first_pass(b, i, half, 1)
-                nc.vector.tensor_tensor(h[b, i][:, js], sums[b, i, half][:], h[b, i][:, js], ALU.mult)
-            if i == 0:
-                looks[b] = sb([P, PACK, M], F32, "table", 2)
+        def look(b, t):
+            for part in parts:
+                if (b, t, part) not in sums:
+                    first_pass(b, t, part, 0)
+                first_pass(b, t, part, 1)
+                cols = h[b, t][:, BANK * part : BANK * (part + 1)]
+                nc.vector.tensor_tensor(cols, sums[b, t, part][:], cols, ALU.mult)
+            if t == 0:
+                looks[b] = sbuf([P, PACK, M], F32, "table", GROUPS)
             nc.scalar.activation(
-                out=looks[b][:, i, :], in_=h[b, i][:].indirect(look_lists[:]), func=ACT.Sigmoid,
-                bias=thr_sb[:, b, i : i + 1], scale=slope_sb[:, b, i : i + 1],
+                out=looks[b][:, t, :],
+                in_=h[b, t][:].indirect(look_lists[:]),
+                func=ACT.Sigmoid,
+                bias=thr_sb[:, b, t : t + 1],
+                scale=slope_sb[:, b, t : t + 1],
             )
 
-        def make_x(b, half, tag):
+        def make_x(b, half):
             ms = slice(HALF * half, HALF * (half + 1))
-            staged = sb([P, PACK * HALF], BF16, tag)
+            staged = stage_tile()
             nc.vector.tensor_tensor(
-                staged[:].rearrange("p (c k i) -> p c i k", i=PACK, k=4),
-                looks[b][:, :, ms].rearrange("p i (c k) -> p c i k", k=4),
-                plan_sb[b][:, :, ms].rearrange("p i (c k) -> p c i k", k=4),
+                staged[:, : PACK * HALF].rearrange("p (c k t) -> p c t k", t=PACK, k=LINE),
+                looks[b][:, :, ms].rearrange("p t (c k) -> p c t k", k=LINE),
+                plan_sb[b][:, :, ms].rearrange("p t (c k) -> p c t k", k=LINE),
                 ALU.mult,
             )
             return staged
 
         open_sums(0, range(PACK))
         look(0, 0)
-        w1q[0, 1] = quantize(round_weight(w1_raw[0, 1], on_vector, wide("w1_00_staged")), GROUP, "w1_01")
-        w2_plane = sb([P, 2 * N], U8, "w2_plane")
-        nc.vector.tensor_copy(
-            w2_plane[:].rearrange("p (u t c) -> p u c t", u=4, t=PACK),
-            w2_plane_raw[:].rearrange("p (u c t) -> p u c t", u=4, t=PACK),
-        )
-        staged = round_weight(w1_raw[1, 1], on_scalar, wide("rows", 8))
+        w1_01 = round_weight(w1_raw[0, 1], on_vector)
         look(0, 1)
         look(0, 2)
-        open_sums(1, range(2))
-        w1q[1, 1] = quantize(staged, GROUP, "w1_11")
+        w1_11 = round_weight(w1_raw[1, 1], on_scalar)
+        w1q[0, 1] = quantize(w1_01, GROUP, "w1_01")
+        w2_plane = sbuf([P, GROUPS * N], U8, "w2_plane")
+        nc.vector.tensor_copy(
+            w2_plane[:].rearrange("p (u t c) -> p u c t", u=GROUPS * GROUPS, t=PACK),
+            w2_plane_raw[:].rearrange("p (u c t) -> p u c t", u=GROUPS * GROUPS, t=PACK),
+        )
+        open_sums(1, range(PACK // 2))
+        w1q[1, 1] = quantize(w1_11, GROUP, "w1_11")
         look(0, 3)
-        look(1, 0)
-        open_sums(1, range(2, PACK))
-        for i in range(1, PACK):
-            look(1, i)
-        staged_w3 = round_weight(w3_raw[0, 0], on_scalar, wide("slope"))
-        for b in range(2):
-            staged = [make_x(b, half, ("w1_11_codes", "v1", "x10", "x11")[2 * b + half]) for half in range(2)]
-            for half in range(2):
-                xq[b, half] = quantize(staged[half], HALF, f"x_{b}{half}")
+        for t in range(PACK):
+            look(1, t)
+        halves = range(M // HALF)
+        for b in range(GROUPS):
+            x_staged = [make_x(b, half) for half in halves]
+            for half in halves:
+                xq[b, half] = quantize(x_staged[half], HALF, f"x_{b}{half}")
 
-        y_plane = sb([P, 2, M], U8, "y_plane")
+        y_plane = sbuf([P, GROUPS, M], U8, "y_plane")
         y = {}
+        pairs = range(PACK // 2)
 
-        def second_sums(half, stationary):
-            accs = [psum.tile([P, 2, HALF], F32, name="bank", tag="bank") for pair in range(2)]
-            for a in range(2):
-                codes, plane = xq[a, half]
-                for t in range(PACK):
-                    w_codes, w_plane = stationary(a, t)
-                    nc.tensor.matmul_mx(
-                        out=accs[t // 2][:, t % 2, :], lhsT=w_codes, lhsT_scale=w_plane,
-                        rhs=codes[:].bitcast(FP8X4), rhs_scale=plane[:],
-                        start=(a == 0 and t % 2 == 0), stop=(a == 1 and t % 2 == 1),
-                    )
-            return accs
+        def unit_tile():
+            return row_tile()[:].rearrange("p (t m) -> p t m", t=PACK)
 
-        def phase(g, half, angle):
+        def phase(g, half):
             ms = slice(HALF * half, HALF * (half + 1))
-
-            def w2_columns(a, t):
-                col = N * a + GROUP * g + P * t
-                return w2_codes[:, 2 * col : 2 * (col + P)].bitcast(FP4X4), w2_plane[:, col : col + P]
-
-            accs = second_sums(half, w2_columns)
-            for pair in range(2):
-                ts = slice(2 * pair, 2 * pair + 2)
-                nc.vector.scalar_tensor_tensor(
-                    angle[:, ts, :], accs[pair][:], math.pi / 2, weather_sb[g][:, ts, ms], ALU.add, ALU.add
-                )
-            y[g, half] = sb([P, PACK, HALF], F32, "rows", 8)
-            nc.scalar.activation(out=y[g, half][:], in_=angle[:, :, :], func=ACT.Sin, scale=0.5)
-            nc.scalar.activation(out=y[g, half][:], in_=y[g, half][:], func=ACT.Square, scale=math.sqrt(2.0))
+            for pair in pairs:
+                acc = psum.tile([P, 2, HALF], F32, name="bank", tag="bank")
+                for side in range(2):
+                    for a in range(GROUPS):
+                        col = N * a + GROUP * g + P * (2 * pair + side)
+                        codes, plane = xq[a, half]
+                        nc.tensor.matmul_mx(
+                            out=acc[:, side, :],
+                            lhsT=w2_codes[:, 2 * col : 2 * (col + P)].bitcast(FP4X4),
+                            lhsT_scale=w2_plane[:, col : col + P],
+                            rhs=codes[:].bitcast(FP8X4),
+                            rhs_scale=plane[:],
+                            start=(a == 0),
+                            stop=(a == GROUPS - 1),
+                        )
+                rows = angle[g][:, 2 * pair : 2 * pair + 2, ms]
+                nc.vector.scalar_tensor_tensor(rows, acc[:], math.pi / 2, rows, ALU.add, ALU.add)
+            sines = unit_tile()
+            nc.scalar.activation(out=sines, in_=angle[g][:, :, ms], func=ACT.Sin, scale=0.5)
+            y[g, half] = unit_tile()
+            nc.scalar.activation(out=y[g, half], in_=sines, func=ACT.Square, scale=math.sqrt(2.0))
 
         def amplitude(g, half):
-            ms = slice(HALF * half, HALF * (half + 1))
-
-            def w3_columns(a, t):
-                codes, plane = w3q[a, g]
-                return codes[:, P * t : P * (t + 1)].bitcast(FP8X4), plane[:, P * t : P * (t + 1)]
-
-            accs = second_sums(half, w3_columns)
-            for pair in range(2):
+            accs = [psum.tile([P, 2, HALF], F32, name="bank", tag="bank") for pair in pairs]
+            for a in range(GROUPS):
+                w_codes, w_plane = w3q[a, g]
+                codes, plane = xq[a, half]
+                for t in range(PACK):
+                    cols = slice(P * t, P * (t + 1))
+                    nc.tensor.matmul_mx(
+                        out=accs[t // 2][:, t % 2, :],
+                        lhsT=w_codes[:, cols].bitcast(FP8X4),
+                        lhsT_scale=w_plane[:, cols],
+                        rhs=codes[:].bitcast(FP8X4),
+                        rhs_scale=plane[:],
+                        start=(a == 0 and t % 2 == 0),
+                        stop=(a == GROUPS - 1 and t % 2 == 1),
+                    )
+            for pair in pairs:
                 rows = y[g, half][:, 2 * pair : 2 * pair + 2, :]
                 nc.vector.scalar_tensor_tensor(rows, rows, 1.0, accs[pair][:], ALU.subtract, ALU.mult)
-            nc.sync.dma_start(dealt_rows(out_0, g)[:, :, ms], y[g, half][:])
+            nc.sync.dma_start(by_word(out_0, g)[:, :, HALF * half : HALF * (half + 1)], y[g, half])
 
         def planes(g, half, copy):
             ms = slice(HALF * half, HALF * (half + 1))
-            staged = sb([P, PACK * HALF], BF16, "y_staged", 2)
+            staged = stage_tile()
             copy(
-                staged[:].rearrange("p (c k t) -> p c t k", t=PACK, k=4),
-                y[g, half][:].rearrange("p t (c k) -> p c t k", k=4),
+                staged[:, : PACK * HALF].rearrange("p (c k t) -> p c t k", t=PACK, k=LINE),
+                y[g, half].rearrange("p t (c k) -> p c t k", k=LINE),
             )
-            codes = sb([P, HALF], U32, "y_codes", 4)
-            nc.vector.quantize_mx(out=codes[:].bitcast(FP8X4), scales=y_plane[:, g, ms], in_=staged[:])
+            codes = sbuf([P, HALF], U32, f"y_codes{g}{half}")
+            nc.vector.quantize_mx(
+                out=codes[:].bitcast(FP8X4), scales=y_plane[:, g, ms], in_=staged[:, : PACK * HALF]
+            )
             nc.sync.dma_start(out_1[g].rearrange("p m t -> p (m t)").bitcast(I32)[:, ms], codes[:].bitcast(I32))
 
-        w3q[0, 0] = quantize(staged_w3, GROUP, "w3_00")
-        phase(0, 0, sb([P, PACK, HALF], F32, "rows", 8))
-        phase(0, 1, sb([P, PACK, HALF], F32, "angle01"))
-        staged = round_weight(w3_raw[1, 0], on_vector, wide("weather", 2))
-        staged_w3 = round_weight(w3_raw[0, 1], on_scalar, wide("angle01"))
-        w3q[1, 0] = quantize(staged, GROUP, "w3_10")
-        angles = sb([P, 2, PACK, HALF], F32, "w3_10_raw")
-        phase(1, 0, angles[:, 0])
-        phase(1, 1, angles[:, 1])
-        amplitude(0, 0)
-        amplitude(0, 1)
-        staged = round_weight(w3_raw[1, 1], on_vector, wide("weather", 2))
-        w3q[0, 1] = quantize(staged_w3, GROUP, "w3_01")
-        w3q[1, 1] = quantize(staged, GROUP, "w3_11")
+        w3_00 = round_weight(w3_raw[0, 0], on_scalar)
+        for half in halves:
+            phase(0, half)
+        w3q[0, 0] = quantize(w3_00, GROUP, "w3_00")
+        w3_10 = round_weight(w3_raw[1, 0], on_vector)
+        w3_01 = round_weight(w3_raw[0, 1], on_scalar)
+        w3q[1, 0] = quantize(w3_10, GROUP, "w3_10")
+        for half in halves:
+            phase(1, half)
+        for half in halves:
+            amplitude(0, half)
+        w3_11 = round_weight(w3_raw[1, 1], on_vector)
+        w3q[0, 1] = quantize(w3_01, GROUP, "w3_01")
+        w3q[1, 1] = quantize(w3_11, GROUP, "w3_11")
         planes(0, 0, on_vector)
         planes(0, 1, on_scalar)
-        amplitude(1, 0)
-        amplitude(1, 1)
+        for half in halves:
+            amplitude(1, half)
         planes(1, 0, on_scalar)
         planes(1, 1, on_vector)
-        for q in range(QUADRANTS):
-            (nc.scalar if q % 2 else nc.sync).dma_start(
-                out_2[:, 4 * q : 4 * q + 4, :].bitcast(I32).rearrange("g r m -> r g m"),
-                y_plane[32 * q : 32 * q + 4, :, :].bitcast(I32),
+
+        for quadrant in range(QUADRANTS):
+            nc.scalar.dma_start(
+                out_2[:, scale_rows(quadrant), :].bitcast(I32).rearrange("g r m -> r g m"),
+                live_rows(y_plane, quadrant).bitcast(I32),
             )

import math
from contextlib import ExitStack

import concourse.mybir as mybir

K, H, N, T, S, M = 1024, 1024, 1024, 4096, 1024, 512
FLOPS = 2 * K * H * S + 2 * 2 * H * N * M

F32 = mybir.dt.float32
BF16 = mybir.dt.bfloat16
I32 = mybir.dt.int32
U32 = mybir.dt.uint32
U16 = mybir.dt.uint16
U8 = mybir.dt.uint8
FP8X4 = mybir.dt.float8_e4m3fn_x4
FP4X4 = mybir.dt.float4_e2m1fn_x4
ALU = mybir.AluOpType
ACT = mybir.ActivationFunctionType

P = 128
PACK = 4
GROUP = P * PACK
GROUPS = 2
BANK = 512
HALF = M // 2
QUADRANTS = 4
BLOCKS = 4
LIST_ROWS = 16
LINE = 4
RAW_BUFS = 6
STAGE_BUFS = 6


def tile_list_pass_tile_scores_kernel(
    tc, tab_words, tab_scales, offs, offs2, w1, sky, slope, thr, plan,
    w2_words, w2_scales, weather, w3, out_0, out_1, out_2,
):
    nc = tc.nc
    with ExitStack() as ctx:
        keep = ctx.enter_context(tc.tile_pool(name="keep", bufs=1))
        psum = ctx.enter_context(tc.psum_pool(name="psum", bufs=8))

        def sbuf(shape, dtype, tag, bufs=1):
            return keep.tile(shape, dtype, name=tag, tag=tag, bufs=bufs, align_bytes=64)

        def by_word(matrix, g):
            return matrix[GROUP * g : GROUP * (g + 1), :].rearrange("(p t) c -> p t c", t=PACK)

        def live_rows(plane, quadrant, start=0):
            return plane[32 * quadrant + start : 32 * quadrant + start + BLOCKS]

        def scale_rows(quadrant):
            return slice(BLOCKS * quadrant, BLOCKS * (quadrant + 1))

        pass_list = keep.tile([P, S // LIST_ROWS], U16, name="pass_list")
        nc.sync.dma_start(pass_list[:], offs)
        look_lists = keep.tile([P, M // LIST_ROWS], U16, name="look_lists")
        nc.sync.dma_start(look_lists[:], offs2)

        tab_plane = sbuf([P, T], U8, "tab_plane")
        nc.vector.memset(tab_plane[:].bitcast(I32), 0)
        slope_sb = keep.tile([P, GROUPS, PACK], F32, name="slope_sb")
        nc.sync.dma_start(slope_sb[:], slope.rearrange("(b p t) -> p b t", b=GROUPS, t=PACK))
        thr_sb = keep.tile([P, GROUPS, PACK], F32, name="thr_sb")
        nc.sync.dma_start(thr_sb[:], thr.rearrange("(b p t) -> p b t", b=GROUPS, t=PACK))
        w2_plane_raw = sbuf([P, GROUPS * N], U8, "w2_plane_raw")
        nc.gpsimd.memset(w2_plane_raw[:].bitcast(I32), 0)

        w2_raw = sbuf([P, GROUPS * 2 * N], U8, "w2_raw")
        for a in range(GROUPS):
            nc.sync.dma_start(w2_raw[:, 2 * N * a : 2 * N * (a + 1)].bitcast(I32), w2_words[a].bitcast(I32))

        def load_table(a, pieces):
            words = sbuf([P, T], I32, "table", GROUPS)
            src = tab_words[a].rearrange("p n i -> p (n i)").bitcast(I32)
            for u in range(pieces):
                cols = slice(u * T // pieces, (u + 1) * T // pieces)
                nc.sync.dma_start(words[:, cols], src[:, cols])
            return words

        def load_table_scales(a):
            for quadrant in range(QUADRANTS):
                nc.sync.dma_start(
                    live_rows(tab_plane, quadrant, BLOCKS * a).bitcast(I32),
                    tab_scales[a, scale_rows(quadrant), :].bitcast(I32),
                )

        def load_w2_scales():
            for quadrant in range(QUADRANTS):
                nc.sync.dma_start(
                    live_rows(w2_plane_raw, quadrant).bitcast(I32).rearrange("r (a n) -> r a n", a=GROUPS),
                    w2_scales[:, scale_rows(quadrant), :].bitcast(I32).rearrange("a r n -> r a n"),
                )

        def load_weight(w, a, g):
            raw = sbuf([P, PACK, GROUP], F32, "w_raw", RAW_BUFS)
            nc.sync.dma_start(raw[:], by_word(w, a)[:, :, GROUP * g : GROUP * (g + 1)])
            return raw

        def row_tile():
            return sbuf([P, S], F32, "rows", GROUPS * PACK)

        def load_sky(b, t):
            rows = row_tile()
            nc.sync.dma_start(rows[:], by_word(sky, b)[:, t, :])
            return rows

        def load_group(matrix, g, tag):
            rows = sbuf([P, PACK, M], F32, tag, GROUPS)
            nc.sync.dma_start(rows[:], by_word(matrix, g))
            return rows

        table, w1_raw, w3_raw, h, plan_sb, angle = {}, {}, {}, {}, {}, {}
        table[0] = load_table(0, 2)
        load_table_scales(0)
        w1_raw[0, 0] = load_weight(w1, 0, 0)
        load_table_scales(1)
        w1_raw[1, 0] = load_weight(w1, 1, 0)
        table[1] = load_table(1, 1)
        h[0, 0] = load_sky(0, 0)
        h[0, 1] = load_sky(0, 1)
        w1_raw[0, 1] = load_weight(w1, 0, 1)
        load_w2_scales()
        w1_raw[1, 1] = load_weight(w1, 1, 1)
        h[0, 2] = load_sky(0, 2)
        h[0, 3] = load_sky(0, 3)
        for t in range(PACK):
            h[1, t] = load_sky(1, t)
        for b in range(GROUPS):
            plan_sb[b] = load_group(plan, b, "plan")
        w3_raw[0, 0] = load_weight(w3, 0, 0)
        angle[0] = load_group(weather, 0, "angle")
        w3_raw[1, 0] = load_weight(w3, 1, 0)
        angle[1] = load_group(weather, 1, "angle")
        w3_raw[0, 1] = load_weight(w3, 0, 1)
        w3_raw[1, 1] = load_weight(w3, 1, 1)

        on_scalar, on_vector = nc.scalar.copy, nc.vector.tensor_copy

        def stage_tile():
            return sbuf([P, PACK * GROUP], BF16, "stage", STAGE_BUFS)

        def round_weight(raw, copy):
            staged = stage_tile()
            copy(
                staged[:].rearrange("p (t c j) -> p c j t", t=PACK, j=PACK),
                raw[:].rearrange("p j (c t) -> p c j t", t=PACK),
            )
            return staged

        def quantize(staged, width, tag):
            codes = sbuf([P, width], U32, tag + "_codes")
            plane = sbuf([P, width], U8, tag + "_plane")
            nc.vector.quantize_mx(out=codes[:].bitcast(FP8X4), scales=plane[:], in_=staged[:, : PACK * width])
            return codes, plane

        def gather_words(a, part):
            entries = pass_list[:, part * BANK // LIST_ROWS : (part + 1) * BANK // LIST_ROWS]
            codes = sbuf([P, BANK], U32, f"v{a}{part}")
            nc.vector.tensor_copy(codes[:], table[a][:].bitcast(U32).indirect(entries))
            return codes

        w2_codes = sbuf([P, GROUPS * 2 * N], U8, "w2_codes")
        nc.vector.tensor_copy(
            w2_codes[:].rearrange("p (u t c e) -> p u c t e", u=GROUPS * GROUPS, t=PACK, e=2),
            w2_raw[:].rearrange("p (u c t e) -> p u c t e", u=GROUPS * GROUPS, t=PACK, e=2),
        )

        parts = range(S // BANK)
        w1q, w3q, xq, v_codes = {}, {}, {}, {}
        for part in parts:
            v_codes[0, part] = gather_words(0, part)
        v_plane = sbuf([P, S], U8, "v_plane")
        nc.vector.tensor_copy(v_plane[:], tab_plane[:].indirect(pass_list[:]))
        for a in range(GROUPS):
            w1q[a, 0] = quantize(round_weight(w1_raw[a, 0], on_scalar), GROUP, f"w1_{a}0")
        for part in parts:
            v_codes[1, part] = gather_words(1, part)

        sums, looks = {}, {}

        def first_pass(b, t, part, a):
            cols = slice(P * t, P * (t + 1))
            if a == 0:
                sums[b, t, part] = psum.tile([P, BANK], F32, name="bank", tag="bank")
            codes, plane = w1q[a, b]
            nc.tensor.matmul_mx(
                out=sums[b, t, part][:],
                lhsT=codes[:, cols].bitcast(FP8X4),
                lhsT_scale=plane[:, cols],
                rhs=v_codes[a, part][:].bitcast(FP8X4),
                rhs_scale=v_plane[BLOCKS * a :, BANK * part : BANK * (part + 1)],
                start=(a == 0),
                stop=(a == GROUPS - 1),
            )

        def open_sums(b, slices):
            for t in slices:
                for part in parts:
                    first_pass(b, t, part, 0)

        def look(b, t):
            for part in parts:
                if (b, t, part) not in sums:
                    first_pass(b, t, part, 0)
                first_pass(b, t, part, 1)
                cols = h[b, t][:, BANK * part : BANK * (part + 1)]
                nc.vector.tensor_tensor(cols, sums[b, t, part][:], cols, ALU.mult)
            if t == 0:
                looks[b] = sbuf([P, PACK, M], F32, "table", GROUPS)
            nc.scalar.activation(
                out=looks[b][:, t, :],
                in_=h[b, t][:].indirect(look_lists[:]),
                func=ACT.Sigmoid,
                bias=thr_sb[:, b, t : t + 1],
                scale=slope_sb[:, b, t : t + 1],
            )

        def make_x(b, half):
            ms = slice(HALF * half, HALF * (half + 1))
            staged = stage_tile()
            nc.vector.tensor_tensor(
                staged[:, : PACK * HALF].rearrange("p (c k t) -> p c t k", t=PACK, k=LINE),
                looks[b][:, :, ms].rearrange("p t (c k) -> p c t k", k=LINE),
                plan_sb[b][:, :, ms].rearrange("p t (c k) -> p c t k", k=LINE),
                ALU.mult,
            )
            return staged

        open_sums(0, range(PACK))
        look(0, 0)
        w1_01 = round_weight(w1_raw[0, 1], on_vector)
        look(0, 1)
        look(0, 2)
        w1_11 = round_weight(w1_raw[1, 1], on_scalar)
        w1q[0, 1] = quantize(w1_01, GROUP, "w1_01")
        w2_plane = sbuf([P, GROUPS * N], U8, "w2_plane")
        nc.vector.tensor_copy(
            w2_plane[:].rearrange("p (u t c) -> p u c t", u=GROUPS * GROUPS, t=PACK),
            w2_plane_raw[:].rearrange("p (u c t) -> p u c t", u=GROUPS * GROUPS, t=PACK),
        )
        open_sums(1, range(PACK // 2))
        w1q[1, 1] = quantize(w1_11, GROUP, "w1_11")
        look(0, 3)
        for t in range(PACK):
            look(1, t)
        halves = range(M // HALF)
        for b in range(GROUPS):
            x_staged = [make_x(b, half) for half in halves]
            for half in halves:
                xq[b, half] = quantize(x_staged[half], HALF, f"x_{b}{half}")

        y_plane = sbuf([P, GROUPS, M], U8, "y_plane")
        y = {}
        pairs = range(PACK // 2)

        def unit_tile():
            return row_tile()[:].rearrange("p (t m) -> p t m", t=PACK)

        def phase(g, half):
            ms = slice(HALF * half, HALF * (half + 1))
            for pair in pairs:
                acc = psum.tile([P, 2, HALF], F32, name="bank", tag="bank")
                for side in range(2):
                    for a in range(GROUPS):
                        col = N * a + GROUP * g + P * (2 * pair + side)
                        codes, plane = xq[a, half]
                        nc.tensor.matmul_mx(
                            out=acc[:, side, :],
                            lhsT=w2_codes[:, 2 * col : 2 * (col + P)].bitcast(FP4X4),
                            lhsT_scale=w2_plane[:, col : col + P],
                            rhs=codes[:].bitcast(FP8X4),
                            rhs_scale=plane[:],
                            start=(a == 0),
                            stop=(a == GROUPS - 1),
                        )
                rows = angle[g][:, 2 * pair : 2 * pair + 2, ms]
                nc.vector.scalar_tensor_tensor(rows, acc[:], math.pi / 2, rows, ALU.add, ALU.add)
            sines = unit_tile()
            nc.scalar.activation(out=sines, in_=angle[g][:, :, ms], func=ACT.Sin, scale=0.5)
            y[g, half] = unit_tile()
            nc.scalar.activation(out=y[g, half], in_=sines, func=ACT.Square, scale=math.sqrt(2.0))

        def amplitude(g, half):
            accs = [psum.tile([P, 2, HALF], F32, name="bank", tag="bank") for pair in pairs]
            for a in range(GROUPS):
                w_codes, w_plane = w3q[a, g]
                codes, plane = xq[a, half]
                for t in range(PACK):
                    cols = slice(P * t, P * (t + 1))
                    nc.tensor.matmul_mx(
                        out=accs[t // 2][:, t % 2, :],
                        lhsT=w_codes[:, cols].bitcast(FP8X4),
                        lhsT_scale=w_plane[:, cols],
                        rhs=codes[:].bitcast(FP8X4),
                        rhs_scale=plane[:],
                        start=(a == 0 and t % 2 == 0),
                        stop=(a == GROUPS - 1 and t % 2 == 1),
                    )
            for pair in pairs:
                rows = y[g, half][:, 2 * pair : 2 * pair + 2, :]
                nc.vector.scalar_tensor_tensor(rows, rows, 1.0, accs[pair][:], ALU.subtract, ALU.mult)
            nc.sync.dma_start(by_word(out_0, g)[:, :, HALF * half : HALF * (half + 1)], y[g, half])

        def planes(g, half, copy):
            ms = slice(HALF * half, HALF * (half + 1))
            staged = stage_tile()
            copy(
                staged[:, : PACK * HALF].rearrange("p (c k t) -> p c t k", t=PACK, k=LINE),
                y[g, half].rearrange("p t (c k) -> p c t k", k=LINE),
            )
            codes = sbuf([P, HALF], U32, f"y_codes{g}{half}")
            nc.vector.quantize_mx(
                out=codes[:].bitcast(FP8X4), scales=y_plane[:, g, ms], in_=staged[:, : PACK * HALF]
            )
            nc.sync.dma_start(out_1[g].rearrange("p m t -> p (m t)").bitcast(I32)[:, ms], codes[:].bitcast(I32))

        w3_00 = round_weight(w3_raw[0, 0], on_scalar)
        for half in halves:
            phase(0, half)
        w3q[0, 0] = quantize(w3_00, GROUP, "w3_00")
        w3_10 = round_weight(w3_raw[1, 0], on_vector)
        w3_01 = round_weight(w3_raw[0, 1], on_scalar)
        w3q[1, 0] = quantize(w3_10, GROUP, "w3_10")
        for half in halves:
            phase(1, half)
        for half in halves:
            amplitude(0, half)
        w3_11 = round_weight(w3_raw[1, 1], on_vector)
        w3q[0, 1] = quantize(w3_01, GROUP, "w3_01")
        w3q[1, 1] = quantize(w3_11, GROUP, "w3_11")
        planes(0, 0, on_vector)
        planes(0, 1, on_scalar)
        for half in halves:
            amplitude(1, half)
        planes(1, 0, on_scalar)
        planes(1, 1, on_vector)

        for quadrant in range(QUADRANTS):
            nc.scalar.dma_start(
                out_2[:, scale_rows(quadrant), :].bitcast(I32).rearrange("g r m -> r g m"),
                live_rows(y_plane, quadrant).bitcast(I32),
            )
